import numpy as np, ml_dtypes
CORES = [10,34,74,98]
N = 4
BF = ml_dtypes.bfloat16
def gentries(a):
    return np.ascontiguousarray(a.reshape(8, 16, -1).transpose(0, 2, 1)).reshape(8, -1)
def gtable(e):
    e = np.asarray(e); return np.ascontiguousarray(e.reshape(8, -1, 16).transpose(0, 2, 1)).reshape(128, -1).astype(np.int32)
W, LW, M, K, CAP, RO = 4096, 12, 1024, 256, 128, 4
def h1(v):
    return ((v * v >> 3) + v) & (W - 1)
def h2(v):
    return ((v * v >> 5) + 37 * v + 1) & (W - 1)
def parts(rng):
    X = rng.integers(0, 16, (N, 8, 16, W)); F = rng.integers(0, W, (N, 8, 16, W)); LG = rng.integers(0, M, (N, 8, W))
    for q in range(N):
        for g in range(8):
            v = rng.permutation(M)[:7 * M // 10]
            LG[q, g, np.where(rng.random(len(v)) < 0.5, h1(v), h2(v))] = v
    LE = (rng.random((N, 8, W)) < rng.choice(np.array([0.3, 0.5, 0.7, 0.9]), (N, 8, 1))).astype(np.int64)
    XL = rng.integers(0, 16, (N, 8, 16, M)); LF = rng.integers(0, M, (N, 8, 16, M))
    return X, F, LG, LE, XL, LF, rng.integers(0, W, (N, 8, 16, K)), rng.integers(0, 16, (N, 8, 16, K))
def pack(X, F, LG, LE, XL, LF, C, Q):
    def bf(a): return np.ascontiguousarray(a).reshape(N, 128, -1).astype(np.float32).astype(BF)
    F = np.ascontiguousarray(F).reshape(N, 128, W)
    return {"xr": bf(X), "fd": (F[..., :W // 2] + W * F[..., W // 2:]).astype(np.int32), "tg": (2 * LG + LE).astype(np.int32), "xl": bf(XL),
            "lf": np.ascontiguousarray(LF).reshape(N, 128, M).astype(np.int32), "cx": np.stack([gtable(a.transpose(0, 2, 1).reshape(8, -1)) for a in C]), "qx": bf(Q)}
def setup_inputs(rng):
    return pack(*parts(rng))
def setup_inputs_spread(rng):
    X, F, LG, LE, XL, LF, C, Q = parts(rng)
    def small(n): return np.minimum((np.exp2(4.2 * rng.random((N, 8, 1, n))) * rng.random((N, 8, 16, n))).astype(np.int64), 15)
    def low(n, top): return np.minimum((top * rng.random((N, 8, 16, n)) ** rng.choice(np.array([1.0, 2.0, 4.0]), (N, 8, 1, n))).astype(np.int64), top - 1)
    LE = (rng.random((N, 8, W)) < rng.random((N, 8, 1))).astype(np.int64)
    return pack(small(W), low(W, W), LG, LE, small(M), low(M, M), low(K, W), small(K))
def setup_inputs_ends(rng):
    X, F, LG, LE, XL, LF, C, Q = parts(rng); h = W // 2
    def faces(n):
        kind = rng.integers(0, 3, (N, 8, 1, n)); a = 15 * np.where(kind == 2, rng.integers(0, 2, (N, 8, 16, n)), kind)
        near = (rng.random((N, 8, 1, n)) < 0.25) & (np.arange(16)[:, None] == rng.integers(0, 16, (N, 8, 1, n)))
        return np.abs(a - near.astype(np.int64))
    def ends(a, top): return np.where(rng.random(a.shape) < 0.66, top * rng.integers(0, 2, a.shape), a)
    X, XL, Q = faces(W), faces(M), faces(K)
    X[..., 0] = 0; X[..., W - 1] = 0; X[..., 1] = 15; X[..., W - 2] = 15
    X[..., 2] = 0; X[..., 0, 2] = 1; X[..., W - 3] = 0; X[..., 15, W - 3] = 1
    m = rng.random((N, 8, 16, h)) < 0.66; e = (W - 1) * rng.integers(0, 2, m.shape)
    F = np.concatenate([np.where(m, e, F[..., :h]), np.where(m, e, F[..., h:])], axis=-1)
    m = rng.random((N, 8, W)) < 0.66; e = (rng.random((N, 8, W)) < 0.6).astype(np.int64)
    LG = np.where(m, (M - 1) * e, LG); LE = np.where(m, e, LE)
    LG[..., 0] = 0; LE[..., 0] = 0; LG[..., W - 1] = M - 1; LE[..., W - 1] = 1
    LF = ends(LF, M - 1); C = ends(C, W - 1)
    for k in (0, 1, K - 1): Q[..., k] = 15; C[..., k] = (W - 1) * rng.integers(0, 2, (N, 8, 16))
    Q[..., K - 2] = 0; C[..., K - 2] = (W - 1) * rng.integers(0, 2, (N, 8, 16))
    for k in (2, K - 3): Q[..., k] = 0; C[..., :15, k] = 1; C[..., 15, k] = W - 1
    for k, v in ((3, 2), (K - 4, W - 3)): Q[..., k] = 15; C[..., :15, k] = (W - 1) * rng.integers(0, 2, (N, 8, 15)); C[..., 15, k] = v
    return pack(X, F, LG, LE, XL, LF, C, Q)
def setup_inputs_corners(rng):
    X, F, LG, LE, XL, LF, C, Q = parts(rng); cnt = (0, 1, CAP - 1, CAP, CAP + 1, K); a = np.arange(M)
    for g in (2, 7):
        LG[:, g] = LG[0, g]; res = a[(LG[0, g][h1(a)] == a) | (LG[0, g][h2(a)] == a)]; LF[:, g] = rng.choice(res, (N, 16, M))
    v = LG[:, 3]; c = np.arange(W)
    for _ in range(3): v = np.where((h1(v) == c) | (h2(v) == c), (v + 1) % M, v)
    LG[:, 3] = v
    few = np.array([0, 1, M - 2, M - 1]); LF[:, 5] = rng.choice(few, (N, 16, M)); LG[:, 6] = rng.choice(few, (N, W))
    LE[:, 4] = 1; LE[0, 0] = 0
    for q in range(N):
        for g in range(8):
            b = rng.permutation(W)[:4 * K].reshape(K, 4)
            C[q, g] = b[np.arange(K)[None, :], rng.integers(0, 4, (16, K))]
            ask = np.zeros(K, np.int64); ask[rng.permutation(K)[:cnt[(q + g) % 6]]] = 1
            if g == 7:
                o = C[q, g][np.argmin(far(X[q, g], C[q, g], Q[q, g]), axis=0), np.arange(K)]; LE[q, g] = 0; LE[q, g, o] = ask
            else: LE[q, g, b] = ask[:, None]
    return pack(X, F, LG, LE, XL, LF, C, Q)
def setup_inputs_ties(rng):
    X, F, LG, LE, XL, LF, C, Q = parts(rng)
    pal = rng.integers(6, 10, (N, 8, 16, 6))
    X = np.take_along_axis(pal, rng.integers(0, 6, (N, 8, 1, W)), 3); XL = np.take_along_axis(pal, rng.integers(0, 6, (N, 8, 1, M)), 3)
    for q in range(N):
        for g in range(8):
            v = rng.permutation(M)[:M // 2]; LG[q, g, h2(v)] = v; LG[q, g, h1(v)] = v
    return pack(X, F, LG, LE, XL, LF, C, Q)
def setup_inputs_alike(rng):
    X, F, LG, LE, XL, LF, C, Q = parts(rng)
    for g in range(8):
        s = rng.permutation(M); w = s[:64]; pl = np.concatenate([h1(w), h2(w)])
        pair = s[:6]; few = np.concatenate([pair, pair ^ 1])
        for q in range(N):
            if g % 2 == 0:
                pool = rng.permutation(W)[:40]; C[q, g] = rng.choice(pool, (16, K)); F[q, g, :, ::2] = rng.choice(pool, (16, W // 2))
                LE[q, g, pool] = rng.random(40) < 0.8; LG[q, g, pool] = rng.choice(few, 40); LF[q, g] = rng.choice(s[:24], (16, M))
            else:
                C[q, g] = rng.choice(pl, (16, K)); LE[q, g, pl] = 1; LG[q, g, pl] = rng.choice(s[64:], 128); LF[q, g] = rng.choice(w, (16, M))
    return pack(X, F, LG, LE, XL, LF, C, Q)
def check_inputs(d):
    bad = []
    for k, lo, hi in (("xr", 0, 15), ("fd", 0, W * W - 1), ("tg", 0, 2 * M - 1), ("xl", 0, 15), ("lf", 0, M - 1), ("cx", 0, W - 1), ("qx", 0, 15)):
        a = np.asarray(d[k]).astype(np.float64)
        if not (np.min(a) >= lo and np.max(a) <= hi): bad.append("range of " + k)
        elif np.any(a != np.floor(a)): bad.append("whole numbers of " + k)
    return bad
def lowest(key, use):
    ix = np.flatnonzero(use); m = np.zeros(len(key), bool); m[ix[np.unique(key[ix], return_index=True)[1]]] = True
    return m
def far(x, c, q):
    return np.add.reduce(np.abs(x[:, c] - q[:, None, :]), axis=0)
def reference(xr, fd, tg, xl, lf, cx, qx):
    def whole(a): return a.astype(np.float32).astype(np.int64).reshape(N, 8, 16, -1)
    X, XL, Q = whole(xr), whole(xl), whole(qx)
    fi = fd.astype(np.int64); F = np.concatenate([fi & (W - 1), fi >> LW], axis=-1).reshape(N, 8, 16, W)
    LG = tg.astype(np.int64) >> 1; LE = tg.astype(np.int64) & 1; LF = lf.astype(np.int64).reshape(N, 8, 16, M)
    C = np.ascontiguousarray(np.stack([gentries(a) for a in cx]).astype(np.int64).reshape(N, 8, K, 16).transpose(0, 1, 3, 2))
    lane = np.arange(K)
    for t in range(RO):
        asked = {}; back = {}
        for r in range(N):
            for g in range(8):
                c = C[r, g]; o = c[np.argmin(far(X[r, g], c, Q[r, g]), axis=0), lane]
                s = np.flatnonzero(lowest(o, LE[r, g][o] == 1))[:CAP]
                asked[r, g] = (o, s, LG[r, g][o[s]], LG[r, g][c[:, s]])
        for r in range(N):
            p = (r + 1 + t % (N - 1)) % N
            for g in range(8):
                o, s, n, sent = asked[r, g]
                back[r, g] = (XL[p, g][:, n], LF[p, g][:, n])
                w = lowest(n ^ 1, np.ones(len(n), bool)); LF[p, g][:, (n ^ 1)[w]] = sent[:, w]
        for r in range(N):
            for g in range(8):
                o, s, n, sent = asked[r, g]; a, v = back[r, g]; q = Q[r, g][:, s]; j = np.arange(len(s))
                c1, c2 = h1(v), h2(v); in1 = LG[r, g][c1] == v; in2 = LG[r, g][c2] == v
                sh = np.where(in1, c1, np.where(in2, c2, np.where(far(X[r, g], c2, q) > far(X[r, g], c1, q), c2, c1)))
                new = ~(in1 | in2); i = np.argmax(new, axis=0); pl = sh[i, j]; w = lowest(pl, np.any(new, axis=0))
                LG[r, g][pl[w]] = v[i, j][w]; LE[r, g][pl[w]] = 1
                F[r, g][:, o[s]] = sh; X[r, g][:, o[s]] = a; LE[r, g][o[s]] = 0
                C[r, g] = F[r, g][:, o]; Q[r, g] = (Q[r, g] + X[r, g][:, o]) >> 1
    return {"yc": C.reshape(N, 128, K).astype(np.float32), "yq": Q.reshape(N, 128, K).astype(np.float32).astype(BF), "yt": (2 * LG + LE).astype(np.float32), "yl": LF.reshape(N, 128, M).astype(np.float32)}

@@ -1,0 +1,676 @@
+import numpy as np
+from concourse.mybir import AluOpType as O, AxisListType, ActivationFunctionType as F
+
+STEPS = 4
+CHOICE = "svss"
+CL1, CL2, CU2 = 2, 3, 1
+TRANS = "vsvs"
+SUMV = 5
+
+
+def _scratch():
+    S = {}
+
+    def sb(n, w, d="float32"):
+        S[n] = ("sbuf", [128] + (w if isinstance(w, list) else [w]), d)
+    B, I, U = "bfloat16", "int32", "uint16"
+    sb("V", 4224, B); sb("X0", 4096, B); sb("FW", 4224, I); sb("FD", 2048, I)
+    for k in range(4):
+        sb("LF%d" % k, 1280, I)
+    sb("LFF", 1280, I); sb("LFH", 1024, I); sb("YL", 1280); sb("SD", 128); sb("MD", 8, U)
+    for k in range(3):
+        sb("XL%d" % k, 1152, B)
+    sb("XLH", 1024, B)
+    sb("CI", 256, I); sb("CF", 384); sb("CU", 256, U); sb("Q", 384, B); sb("CE", [16, 16]); sb("CO", [16, 16])
+    for k in range(4):
+        sb("XG%d" % k, 1024, B); sb("XD%d" % k, 1024, B); sb("AB%d" % k, 512, B)
+    for k in range(2):
+        sb("GS%d" % k, 1024, B); sb("SX%d" % k, 1024, B)
+    sb("KEY", [16, 32]); sb("KT", 512); sb("SCN", 512); sb("RST", 512)
+    sb("OI", 16, I); sb("OF", 16); sb("OU", 16, U)
+    sb("VO", 256); sb("XO", 256, B); sb("DD", 384, B); sb("OR", 256, U); sb("EQ", [16, 272], B); sb("CA", 256); sb("PX", 256)
+    sb("ONE", 256); sb("JS", 256, B); sb("JV", 256, B); sb("LS", 8); sb("T2", 1); sb("RL", 8); sb("CBP", 8); sb("INV", 8); sb("H8", 8); sb("LU", 8, U)
+    sb("DDR", 128, B); sb("CR", 128); sb("CRU", 128, U); sb("QR", 128, B)
+    sb("WNF", 8); sb("NU", 8, U); sb("OUR", 8, U); sb("NR", 128, U); sb("A", 128, B); sb("BI", 128, I); sb("BS", 128)
+    sb("SQ", 128, I); sb("S5", 128, I); sb("H", 256, I); sb("CCU", 256, U); sb("D12", 128)
+    sb("IN", 256, B); sb("INB", 128); sb("M2", 128); sb("SEL", 128); sb("SS", 128, I); sb("N12", 128, B); sb("NEW", 128, B)
+    sb("K1", 128); sb("KK", 128); sb("KKE", [8, 16]); sb("KKO", [8, 16]); sb("PEN", [8, 16]); sb("KEC", [8, 32]); sb("KTC", 256); sb("SNC", 256)
+    sb("KI", 8, I); sb("PI", 8, I); sb("BW", 8, I); sb("BU", 8, U); sb("PF", 8); sb("PU", 8, U); sb("P2", 8); sb("PU2", 8, U)
+    sb("GP", 128); sb("XP", 128, B); sb("DP", 128, B); sb("DB", 128, B); sb("ZC", 128, B); sb("NV", 128, B); sb("PLR", 128, U)
+    sb("EQ2", [8, 144], B); sb("FL", 128, B); sb("FS", 8)
+    sb("VL", 128, B); sb("QF", 256); sb("SI", 128, I)
+    sb("NI", 8, I); sb("N1", 8, I); sb("MF", 8); sb("MU", 8, U)
+    sb("YQ", 256, B); sb("TX", 5 * 256, B); sb("TD", 5 * 256, B); sb("TE", 256); sb("TE2", 256); sb("TY", 256); sb("TW", 256)
+    sb("COL", 64); sb("IP", 4, I); sb("BO", 128); sb("BO1", 128); sb("TF4", 80)
+    for n in ("ZK", "ZKN", "ZT", "ZTN", "ZN", "Z1"):
+        sb(n, 144, B)
+    for n in ("ID", "NID", "RN", "RE", "RL128", "RD", "RB", "KEEP", "TRI"):
+        sb(n, 128, B)
+    for n in range(5):
+        sb("TI%d" % n, 128, B); sb("TJ%d" % n, 128, B)
+    sb("ON128", 128); sb("IDF", 128); sb("LTF", 128); sb("J16", 16); sb("POW", 20); sb("DDM", 128, B); sb("CT", 256); sb("CT2", 256)
+    sb("SC8", 8); sb("SW8", 8); sb("SW2", 8); sb("DSC", 8); sb("DSM", 8); sb("CB", 8); sb("I8", 8)
+    sb("TGL", 256, I); sb("NM", 256, I); sb("DI", 9 * 256, I); sb("DG", 9 * 256, B)
+    sb("NB", 64, I); sb("NBD", 256, I); sb("NBB", 320, B); sb("DIG", 1024, B); sb("PJ", 8, I); sb("PJD", 24, I); sb("PD", 40, B)
+    for n in ("ps0", "ps1", "ps2", "ps3", "PA", "PT", "PR", "PC"):
+        S[n] = ("psum", [128, 512], "float32")
+    return S
+
+
+def _pack(S):
+    real, virt, width = {}, {}, {}
+    for n, (where, sh, d) in S.items():
+        if where == "psum" or len(sh) > 2 or sh[1] > 400 or n in ("SD", "MD"):
+            real[n] = (where, sh, d)
+        else:
+            unit = 8 if d in ("float32", "int32") else 16
+            at = width.get(d, 0)
+            virt[n] = ("W" + d, at, sh[1])
+            width[d] = at + -(-sh[1] // unit) * unit
+    for d, w in width.items():
+        real["W" + d] = ("sbuf", [128, w], d)
+    return real, virt
+
+
+ALL = _scratch()
+SCRATCH, VIRT = _pack(ALL)
+ARR = ["ax0", "ax1", "ax2", "af0", "af1", "af2", "af3", "aff", "asd", "amd"]
+SEMAPHORES = ["pv", "pc", "pt", "pg"] + ARR + ["d%d" % k for k in range(70)]
+PSUM = ("ps0", "ps1", "ps2", "ps3", "PA", "PT", "PR", "PC")
+MASKS = {}
+
+
+def rank_program(g, core, T, topo):
+    rank = T.rank_of(core)
+    if rank is None:
+        return
+    eng = {"v": g.vector, "c": g.scalar, "t": g.tensor, "g": g, "y": g.sync}
+    psem = {"v": "pv", "c": "pc", "t": "pt", "g": "pg"}
+    cnt = {"v": 0, "c": 0, "t": 0, "g": 0}
+    know = {q: {} for q in eng}
+    W, R, X = {}, {}, {}
+    total = {}
+    nd = [0]
+
+    def r(name, *idx):
+        key = (name, str(idx))
+        if key not in MASKS:
+            if name in ALL and ALL[name][0] == "sbuf":
+                sh = ALL[name][1][1:]
+                n = int(np.prod(sh)); f = np.zeros(n, np.uint8)
+                f[np.arange(n).reshape(sh)[tuple(idx[1:])].reshape(-1)] = 1
+                MASKS[key] = int.from_bytes(np.packbits(f, bitorder="little").tobytes(), "little")
+            else:
+                MASKS[key] = 1
+        if name in VIRT:
+            arena, at, w = VIRT[name]
+            cs = idx[1] if len(idx) > 1 else slice(0, w)
+            lo, hi, st = cs.indices(w)
+            return (T[arena][idx[0] if idx else slice(None), at + lo:at + hi:st], ((name, MASKS[key]),))
+        t = T[name]
+        return (t[idx] if idx else t[:], ((name, MASKS[key]),))
+
+    def c(name, a, b):
+        return r(name, slice(None), slice(a, b))
+
+    def ind(w, o):
+        return (w[0].indirect(o[0]), w[1] + o[1], w[1])
+
+    def issue(q, fn, outs, ins, dma=None, rows=None):
+        need = []
+        rd = [x for o in ins for x in o[1]]
+        wt = [x for o in outs for x in (o[2] if len(o) > 2 else o[1])]
+        for o in outs:
+            if len(o) > 2:
+                rd += [x for x in o[1] if x not in o[2]]
+        for n, m in rd:
+            if n in PSUM:
+                continue
+            for e in W.get(n, []):
+                if e[0] & m:
+                    need.append(e[1])
+        for n, m in wt:
+            if n in PSUM:
+                continue
+            for e in W.get(n, []):
+                if e[0] & m and not (rows and e[2] == rows):
+                    need.append(e[1])
+            for e in R.get(n, []):
+                if e[0] & m:
+                    need.append(e[1])
+        for n, m in rd + wt:
+            if n in PSUM:
+                need += [tk for q2, tk in X.get(n, {}).items() if q2 != q]
+        best = {}
+        for s, v, sn in need:
+            if s not in best or best[s][0] < v:
+                best[s] = (v, sn)
+        order = sorted(best.items(), key=lambda z: -len(z[1][1]))
+        for s, (v, sn) in order:
+            if know[q].get(s, 0) >= v:
+                continue
+            if any(s2 != s and sn2.get(s, 0) >= v and know[q].get(s2, 0) < v2 for s2, (v2, sn2) in order):
+                continue
+            eng[q].wait_ge(T.sem[s], v)
+            know[q][s] = max(know[q].get(s, 0), v)
+            for a, b in sn.items():
+                if know[q].get(a, 0) < b:
+                    know[q][a] = b
+        inst = fn()
+        if dma is None:
+            cnt[q] += 1
+            tok = (psem[q], cnt[q], dict(know[q]))
+            inst.then_inc(T.sem[psem[q]], 1)
+            total[psem[q]] = cnt[q]
+            mark = q
+        else:
+            tok = (dma[0], dma[1], dict(know[q])); total[dma[0]] = dma[1]; mark = "dma"
+            if dma[2]:
+                inst.then_inc(T.sem[dma[0]], 16)
+        for n, m in rd + wt:
+            if n in PSUM:
+                X.setdefault(n, {})[q] = tok
+        for n, m in wt:
+            if n not in PSUM:
+                W[n] = [(e[0] & ~m, e[1], e[2]) if not (rows and e[2] == rows) else e for e in W.get(n, []) if e[0] & ~m or (rows and e[2] == rows)] + [(m, tok, rows)]
+                R[n] = [(e[0] & ~m, e[1], e[2]) for e in R.get(n, []) if e[0] & ~m]
+        for n, m in rd:
+            if n not in PSUM:
+                R[n] = [e for e in R.get(n, []) if not (e[2] == mark and mark != "dma" and e[0] & ~m == 0)] + [(m, tok, mark)]
+        return tok
+
+    def dma(q, out, in_, accum=False, rows=None):
+        s = "d%d" % nd[0]; nd[0] += 1
+        if accum:
+            issue(q, lambda: eng[q].dma_start(out[0], in_[0], accum_op=O.add, max_dma_last_dim=4096), [out], [in_, out], (s, 16, True))
+        else:
+            issue(q, lambda: eng[q].dma_start(out[0], in_[0]), [out], [in_], (s, 16, True), rows)
+
+    def send(dst, out, in_, rsem):
+        s = "d%d" % nd[0]; nd[0] += 1
+        d = T.cores[dst % 4]
+        rid, pid, _ = topo.addr(d)
+        m = topo.mask(core, d)
+        issue("g", lambda: g.remote_dma(T[out[0]][:, 0:out[1]], in_[0], T.sem[rsem], T.sem[s], pid, rid, m), [], [in_], (s, len(topo.engines(core, d)), False))
+
+    def lands(out, rsem, src):
+        k = len(topo.engines(T.cores[src % 4], core))
+        total[rsem] = k
+        n, m = out[1][0]
+        W[n] = [(e[0] & ~m, e[1], e[2]) for e in W.get(n, []) if e[0] & ~m] + [(m, (rsem, k, {}), None)]
+
+    def ts(o, i, s1, op, s2=None, op2=None):
+        ins = [i] + [s for s in (s1, s2) if isinstance(s, tuple)]
+        a = s1[0] if isinstance(s1, tuple) else s1
+        b = s2[0] if isinstance(s2, tuple) else s2
+        if op2 is None:
+            issue("v", lambda: g.vector.tensor_scalar(o[0], i[0], a, None, op), [o], ins)
+        else:
+            issue("v", lambda: g.vector.tensor_scalar(o[0], i[0], a, b, op, op2), [o], ins)
+
+    def tt(o, a, b, op):
+        issue("v", lambda: g.vector.tensor_tensor(o[0], a[0], b[0], op), [o], [a, b])
+
+    def cp(o, i):
+        issue("v", lambda: g.vector.tensor_copy(o[0], i[0]), [o], [i])
+
+    def ms(o, x):
+        issue("v", lambda: g.vector.memset(o[0], x), [o], [])
+
+    def act(o, i, f=F.Identity, bias=0.0, scale=1.0, acc=None):
+        ins = [i] + ([bias] if isinstance(bias, tuple) else [])
+        b = bias[0] if isinstance(bias, tuple) else bias
+        if acc is None:
+            issue("c", lambda: g.scalar.activation(o[0], i[0], f, bias=b, scale=scale), [o], ins)
+        else:
+            issue("c", lambda: g.scalar.activation(o[0], i[0], f, bias=b, scale=scale, accum_out=acc[0]), [o, acc], ins)
+
+    def mm(o, l, x, start, stop):
+        issue("t", lambda: g.tensor.matmul(o[0], l[0], x[0], start, stop), [o], [l, x])
+
+    def iota(o, pat, base, cm, f=False):
+        if f:
+            issue("g", lambda: g.iota(o[0], pat, base, cm, allow_small_or_imprecise_dtypes=True), [o], [])
+        else:
+            issue("g", lambda: g.iota(o[0], pat, base, cm), [o], [])
+
+    def aff(o, i, pat, base, cm, op=O.is_ge):
+        issue("g", lambda: g.affine_select(o[0], i[0], pat, op, 0.0, base, cm), [o], [i])
+
+    def gat(q, o, w, l, add=None):
+        if q == "v":
+            if add is None:
+                cp(o, ind(w, l))
+            else:
+                ts(o, ind(w, l), add, O.add)
+        else:
+            act(o, ind(w, l), F.Identity, 0.0 if add is None else add)
+
+    def scan(o, d0, d1, init, o0, o1):
+        issue("v", lambda: g.vector.tensor_tensor_scan(o[0], d0[0], d1[0], init, o0, o1), [o], [d0, d1])
+
+    def trn(o, i):
+        issue("v", lambda: g.vector.transpose(o[0], i[0]), [o], [i])
+
+    def col(k):
+        return c("COL", k, k + 1)
+
+    def sel(z, a):
+        return c(z, 15 - a, 143 - a)
+
+    def stp(n, lo, hi, step):
+        return r(n, slice(None), slice(lo, hi, step))
+    A_ = slice(None)
+    SHR, AND = O.logical_shift_right, O.bitwise_and
+
+    dma("y", r("CI"), r("cx")); dma("c", r("TGL"), r("tg")); dma("y", r("X0"), r("xr")); dma("c", c("YQ", 0, 256), r("qx"))
+
+    iota(c("IP", 0, 1), [[1, 1]], 0, 1)
+    iota(r("NM"), [[1, 256]], 0, 256)
+    iota(r("J16"), [[1, 16]], 0, 0, True)
+    iota(r("I8"), [[16, 8]], 0, 0, True)
+    ms(r("ON128"), 1.0)
+    ms(r("V"), 0.0)
+    for j in range(4):
+        ts(c("DI", (5 + j) * 256, (6 + j) * 256), r("NM"), 3 * j, SHR, 7, AND)
+    ts(c("DG", 1280, 2304), c("DI", 1280, 2304), 0.0625, O.mult)
+    for j in range(4):
+        ts(c("DI", j * 256, (j + 1) * 256), r("TGL"), 1 + 3 * j, SHR, 7, AND)
+    ts(c("DI", 1024, 1280), r("TGL"), 1, AND)
+    ts(c("DG", 0, 1280), c("DI", 0, 1280), 0.0625, O.mult)
+    for f in (5, 6, 7, 8, 0, 1, 2, 3, 4):
+        dma("y", r("V", slice(f, None, 16), slice(0, 4096)), c("DG", f * 256, f * 256 + 256), rows="V")
+    aff(r("BO1"), r("ON128"), [[-16, 8], [0, 16]], 0, 1)
+    aff(r("BO"), r("BO1"), [[16, 8], [0, 16]], 15, -1)
+    aff(r("IDF"), r("ON128"), [[-1, 128]], 0, 1, O.is_equal)
+    aff(r("LTF"), r("BO"), [[1, 128]], -1, -1)
+    iota(r("NB"), [[1, 64]], 0, 64)
+    iota(r("PJ"), [[1, 8]], 0, 8)
+    iota(c("CB", 0, SUMV), [[16, SUMV]], 256, 0, True)
+    iota(c("CB", SUMV, 8), [[32, 8 - SUMV]], 32 * SUMV, 0, True)
+    dma("y", r("LFH"), r("lf")); dma("y", r("XLH"), r("xl")); dma("y", r("FD"), r("fd"))
+    dma("g", c("V", 0, 4096), r("xr"), True)
+    for src, b, s in ((1, "XL0", "ax0"), (2, "XL1", "ax1"), (3, "XL2", "ax2")):
+        lands(c(b, 0, 1024), s, rank + src)
+    for src, b, s, w in ((1, "LF0", "af0", 1024), (1, "LF1", "af1", 1024), (1, "LF2", "af2", 1024), (2, "LF3", "af3", 1024), (1, "LFF", "aff", 1024), (3, "SD", "asd", 128), (3, "MD", "amd", 8)):
+        lands(c(b, 0, w), s, rank + src)
+    send(rank + 3, ("LF0", 1024), r("LFH"), "af0")
+    send(rank + 3, ("XL0", 1024), r("XLH"), "ax0")
+    send(rank + 2, ("XL1", 1024), r("XLH"), "ax1")
+    send(rank + 1, ("XL2", 1024), r("XLH"), "ax2")
+    cp(r("CU"), r("CI"))
+    cp(c("CF", 0, 256), r("CI"))
+    ts(c("Q", 0, 256), c("YQ", 0, 256), 192.0, O.add)
+    ms(c("Q", 256, 384), 192.0); ms(c("CF", 256, 384), 0.0)
+    ts(c("IP", 1, 2), c("IP", 0, 1), 15, AND)
+    ts(c("IP", 2, 3), c("IP", 0, 1), 4, SHR, 1, AND)
+    cp(col(0), c("IP", 1, 2)); cp(col(1), c("IP", 2, 3))
+    B24 = 16777216.0
+    ts(col(20), col(1), B24, O.mult)
+    ts(col(21), col(1), -B24, O.mult, B24, O.add)
+    ts(col(24), col(0), 4096.0, O.mult)
+    tt(col(2), col(24), col(20), O.add); tt(col(3), col(24), col(21), O.add)
+
+    def total_of(o, a, b):
+        tmp = c("TF4", 32, 32 + int(a[0].shape[1]))
+        tt(tmp, a, b, O.mult)
+        issue("v", lambda: g.vector.tensor_reduce(o[0], tmp[0], AxisListType.X, O.add), [o], [tmp])
+
+    def scaled(o, i, w):
+        if isinstance(w, tuple):
+            issue("c", lambda: g.scalar.activation(o[0], i[0], F.Copy, scale=w[0]), [o], [i, w])
+        else:
+            act(o, i, F.Copy, 0.0, float(w))
+
+    def zbuf(n, w):
+        scaled(stp(n, 15, 143, 16), stp("BO", 0, 128, 16), w)
+    for n in ("ZK", "ZKN", "ZT", "ZTN", "ZN", "Z1"):
+        ms(r(n), 0.0)
+    scaled(r("ID"), r("IDF"), 1.0); scaled(r("NID"), r("IDF"), -1.0)
+    zbuf("ZK", 65536)
+
+    def consts():
+        ts(c("TF4", 0, 16), r("J16"), col(0), O.is_equal)
+        ms(c("TF4", 16, 32), 0.5); ms(c("TF4", 64, 80), 0.0)
+        scan(c("POW", 0, 16), c("TF4", 16, 32), c("TF4", 64, 80), 65536.0, O.mult, O.add)
+        for j in range(4):
+            ms(c("POW", 16 + j, 17 + j), 16.0 * 8 ** j)
+        total_of(col(4), c("TF4", 0, 4), c("POW", 16, 20)); total_of(col(5), c("TF4", 5, 9), c("POW", 16, 20)); total_of(col(7), c("TF4", 0, 16), c("POW", 0, 16))
+        ts(col(6), c("TF4", 4, 5), -B24, O.mult)
+        ts(col(9), col(0), 5.0, O.is_ge); ts(col(10), col(0), 4.0, O.not_equal)
+        ts(c("COL", 11, 15), c("J16", 1, 5), c("TF4", 4, 5), O.mult, -0.0625, O.mult)
+        ts(c("COL", 15, 19), c("J16", 2, 6), c("TF4", 4, 5), O.mult, -0.0625, O.mult)
+        ts(col(19), col(4), -1.0, O.mult)
+        ms(r("RST"), 0.0); ms(stp("RST", 0, 512, 32), 67108864.0)
+        zbuf("ZN", col(5)); zbuf("ZT", col(4)); zbuf("ZTN", col(19)); zbuf("ZKN", -65536); zbuf("Z1", 0.0625)
+        for n, w in (("RN", col(5)), ("RE", col(6)), ("RL128", col(4)), ("RD", col(7)), ("RB", 65536.0)):
+            scaled(r(n), r("BO"), w)
+        scaled(r("KEEP"), r("IDF"), col(9)); scaled(r("K1"), r("IDF"), -16.0)
+        tt(r("TRI"), r("LTF"), r("K1"), O.add)
+        ts(c("CT2", 0, 16), c("POW", 0, 16), 2.0, O.mult)
+        for k in (16, 32, 64, 128):
+            cp(c("CT2", k, 2 * k), c("CT2", 0, k))
+        act(r("CT"), r("CT2"), F.Copy, -1048576.0)
+
+    def consts2():
+        ts(r("SW8"), r("I8"), col(0), O.add); ts(r("SC8"), r("SW8"), 0.5, O.add); ts(r("SW2"), r("SW8"), 2.0, O.mult)
+        ts(r("DSC"), r("SW8"), 4096.0, O.add); ts(r("DSM"), r("SW8"), 1152.0, O.add)
+        ms(r("ONE"), 1.0)
+        for j in range(3):
+            ts(c("PJD", 8 * j, 8 * j + 8), r("PJ"), 3 * j, SHR, 7 if j < 2 else 1, AND)
+        ts(c("PD", 0, 24), r("PJD"), 0.0625, O.mult)
+        ms(c("PD", 24, 32), 0.125); ms(c("PD", 32, 40), 0.5)
+        ms(c("DD", 256, 384), 0.0)
+        for f, k in ((0, 0), (1, 1), (2, 2), (3, 3), (5, 0), (6, 1), (7, 2), (8, 4)):
+            dma("y", r("DD", slice(f, None, 16), slice(256, 384)), c("PD", 8 * k, 8 * k + 8), rows="DD")
+        for k in range(4):
+            ms(c("LF%d" % k, 1024, 1280), 0)
+        for k in range(3):
+            ms(c("XL%d" % k, 1024, 1152), 0.0)
+        ts(r("NB"), r("NB"), 1023, AND)
+        for j in range(4):
+            ts(c("NBD", 64 * j, 64 * j + 64), r("NB"), 3 * j, SHR, 7, AND)
+        ts(c("NBB", 0, 256), r("NBD"), 0.0625, O.mult)
+        ms(c("NBB", 256, 320), 0.0625)
+        ms(r("DIG"), 0.0)
+        for f in range(5):
+            dma("y", r("DIG", slice(f, None, 16)), c("NBB", 64 * f, 64 * f + 64), rows="DIG")
+        act(c("V", 4096, 4224), c("DD", 256, 384))
+        ms(c("FW", 4096, 4224), 0)
+
+    pk = [0]
+
+    def sub(x, q, lo, u):
+        k = pk[0] % 4; pk[0] += 1
+        for ii in range(8):
+            o = c("ps%d" % k, ii * 64, ii * 64 + 64)
+            mm(o, r("NID"), c(q, lo, lo + 64), True, False)
+            mm(o, r("ID"), stp(x, 8 * u + ii, 1024, 16), False, True)
+        act(r("AB%d" % k), r("ps%d" % k), F.Abs)
+        return k
+
+    def sums(k, z, o, u, first, last):
+        for ii in range(8):
+            mm(o, sel(z, 8 * u + ii), c("AB%d" % k, ii * 64, ii * 64 + 64), first and u == 0 and ii == 0, last and u == 1 and ii == 7)
+
+    def tags(o, gx, xd):
+        for i in range(16):
+            mm(o, sel("ZT", i), stp(gx, i, 1024, 16), i == 0, False)
+            mm(o, sel("ZTN", i), stp(xd, i, 1024, 16), False, i == 15)
+
+    def earlier(eq, row, cols, nb, n):
+        for b in range(nb):
+            ts(r(eq, A_, b, slice(0, n - 16 * b)), c(row, 16 * b, n), c(cols, b, b + 1), O.is_equal)
+
+    def dup_compare(row, cols):
+        earlier("EQ2", row, cols, 8, 128)
+
+    def dup_count():
+        mm(c("PC", 0, 128), r("RD"), r("EQ2", A_, A_, slice(0, 16)), True, False)
+        for b in range(7):
+            mm(c("PC", 16 * b + 16, 128), r("RB"), r("EQ2", A_, b, slice(16, 128 - 16 * b)), False, b == 6)
+
+    def dup_flag(o):
+        tt(o, c("PC", 0, 128), c("CT2", 0, 128), O.is_ge)
+
+    def wrap(o, z, x):
+        for a in range(16):
+            mm(o, sel(z, a), stp(x, a, 128, 16), a == 0, a == 15)
+
+    def choice(t):
+        win = r("X0") if t == 0 else c("V", 0, 4096)
+
+        def take(k):
+            gat("v" if CHOICE[k] == "v" else "c", r("XG%d" % k), win, c("CU", 64 * k, 64 * k + 64), 192.0)
+        order = [k for k in range(4) if CHOICE[k] == "v"] + [k for k in range(4) if CHOICE[k] != "v"]
+        late = order[-1] if CHOICE.count("v") < 3 else None
+        for k in order:
+            if k != late:
+                take(k)
+        if t:
+            disk_write(t - 1)
+            claims2(t - 1)
+        lag = None
+        for n, k in enumerate(order):
+            for u in range(2):
+                b = sub("XG%d" % k, "Q", 64 * k, u)
+                if n == 0 and u == 1 and late is not None:
+                    take(late)
+                if lag:
+                    sums(*lag)
+                lag = (b, "ZK", c("PA", 64 * k, 64 * k + 64), u, True, True)
+                if t and n == CL2 and u == CU2:
+                    claims4(t - 1)
+            if t and n == CL1:
+                claims3(t - 1)
+        act(r("CE"), c("CF", 0, 256), F.Identity, col(2)); act(r("CO"), c("CF", 0, 256), F.Identity, col(3))
+        sums(*lag)
+        if t == 0:
+            consts()
+            consts2()
+        if t:
+            wrap(c("PC", 272, 280), "Z1", "FL")
+
+    def pick(t):
+        tt(r("KEY", A_, A_, slice(0, 16)), c("PA", 0, 256), r("CE"), O.add)
+        tt(r("KEY", A_, A_, slice(16, 32)), c("PA", 0, 256), r("CO"), O.add)
+        trn(r("KT"), r("KEY"))
+        scan(r("SCN"), r("RST"), r("KT"), 67108864.0, O.max, O.min)
+        cp(r("OI"), stp("SCN", 31, 512, 32))
+        ts(r("OI"), r("OI"), 4095, AND)
+        cp(r("OU"), r("OI"))
+        cp(r("OF"), r("OI"))
+        if t:
+            claims5(t - 1)
+        gat("c", r("VO"), r("V"), r("OU"), 192.0)
+        gat("v", r("XO"), r("V"), r("OU"), 192.0)
+        tt(c("DD", 0, 256), r("VO"), r("XO"), O.subtract)
+        mm(c("PR", 0, 256), r("RN"), c("DD", 0, 256), True, True)
+        mm(c("PC", 0, 256), r("RE"), c("DD", 0, 256), True, False)
+        cp(r("OR"), c("PR", 0, 256))
+        for b in range(16):
+            ts(r("EQ", A_, b, slice(0, 256 - 16 * b)), c("OR", 16 * b, 256), c("OF", b, b + 1), O.is_equal)
+            if b < 15:
+                mm(c("PC", 16 * b + 16, 256), r("RB"), r("EQ", A_, b, slice(16, 256 - 16 * b)), False, False)
+        mm(c("PC", 0, 256), r("RD"), r("EQ", A_, A_, slice(0, 16)), False, True)
+        tt(r("CA"), c("PC", 0, 256), r("CT"), O.is_lt)
+        scan(r("PX"), r("ONE"), r("CA"), 0.0, O.mult, O.add)
+        for b in range(SUMV):
+            act(c("JS", 0, 256 - 16 * b), c("PX", 16 * b, 256), F.Sign, c("SC8", b, b + 1), -1.0, c("LS", b, b + 1))
+        ts(r("T2"), c("PX", 255, 256), 2.0, O.mult)
+        for b in range(SUMV, 8):
+            ts(c("JV", 0, 256 - 16 * b), c("PX", 16 * b, 256), c("SC8", b, b + 1), O.is_le, 2.0, O.mult)
+            o, i = c("LS", b, b + 1), c("JV", 0, 256 - 16 * b)
+            issue("v", lambda: g.vector.tensor_reduce(o[0], i[0], AxisListType.X, O.add), [o], [i])
+        ts(r("RL"), r("SW2"), r("T2"), O.subtract, 0.0, O.max)
+        tt(r("CBP"), r("CB"), r("RL"), O.add)
+        ts(r("INV"), r("SW2"), r("T2"), O.is_ge, 8192.0, O.mult)
+        tt(r("H8"), r("LS"), r("CBP"), O.add)
+        ts(r("LU"), r("H8"), 0.5, O.mult)
+        gat("v", r("DDR"), r("DD"), r("LU"))
+        gat("c", r("CR"), r("CF"), r("LU"))
+        gat("c", r("QR"), r("Q"), r("LU"))
+        wrap(c("PR", 256, 264), "ZT", "DDR")
+
+    def translate(t):
+        LF, XL = "LF%d" % t, "XL%d" % (t % 3)
+        cp(r("NU"), c("PR", 256, 264))
+        wrap(c("PC", 264, 272), "ZN", "DDR")
+        mm(c("PC", 0, 128), r("RL128"), r("DDR"), True, True)
+        gat("v", r("BI"), r(LF, A_, slice(0, 1152)), r("NU"))
+        tt(r("SQ"), r("BI"), r("BI"), O.mult)
+        cp(r("CRU"), r("CR"))
+        ts(c("H", 0, 128), r("SQ"), 3, SHR)
+        ts(r("S5"), r("SQ"), 5, SHR)
+        ts(c("H", 128, 256), r("BI"), 37.0, O.mult, 1.0, O.add)
+        tt(c("H", 0, 128), c("H", 0, 128), r("BI"), O.add)
+        tt(c("H", 128, 256), c("H", 128, 256), r("S5"), O.add)
+        ts(r("H"), r("H"), 4095, AND)
+        cp(r("CCU"), r("H"))
+        for k in range(2):
+            gat("c", r("GS%d" % k), r("V"), c("CRU", 64 * k, 64 * k + 64))
+        blk = [(0, 0), (0, 1), (1, 0), (1, 1)]
+        done = []
+        for k, (hs, w) in enumerate(blk):
+            lo = 128 * w + 64 * hs
+            gat("v" if TRANS[k] == "v" else "c", r("XG%d" % k), r("V"), c("CCU", lo, lo + 64))
+            dec = [j for j in range(k + 1) if j not in done and (TRANS[j] == "v" or k > j or k == 3)]
+            for j in dec:
+                ts(r("XD%d" % j), r("XG%d" % j), 192.0, O.add)
+                done.append(j)
+            if k == 0:
+                cp(r("OUR"), c("PC", 264, 272))
+                cp(r("NR"), c("PC", 0, 128))
+        gat("c", r("A"), r(XL), r("NU"))
+        lag = []
+        order = [k for k in range(4) if TRANS[k] == "v" and blk[k][0] == 0] + [k for k in range(4) if TRANS[k] != "v" and blk[k][0] == 0]
+        order += [k for k in range(4) if TRANS[k] == "v" and blk[k][0] == 1] + [k for k in range(4) if TRANS[k] != "v" and blk[k][0] == 1]
+
+        bank = [("PC", 128, "PR", 384), ("PT", 0, "PA", 256)]
+
+        def flush(x):
+            k, bs, pos = x
+            hs, w = blk[k]
+            bt, t0, ba, a0 = bank[hs]
+            tags(c(bt, t0 + 64 * w, t0 + 64 * w + 64), "XG%d" % k, "XD%d" % k)
+            for u in range(2):
+                sums(bs[u], "ZK" if w else "ZKN", c(ba, a0, a0 + 64), u, pos == 0, pos == 1)
+
+        def decide(hs):
+            bt, t0, ba, a0 = bank[hs]
+            lo, hi = 64 * hs, 64 * hs + 64
+            for w in range(2):
+                tt(c("IN", 128 * w + lo, 128 * w + hi), c(bt, t0 + 64 * w, t0 + 64 * w + 64), c("BS", lo, hi), O.is_equal)
+            ts(c("INB", lo, hi), c("IN", lo, hi), 33554432.0, O.mult)
+            tt(c("M2", lo, hi), c(ba, a0, a0 + 64), c("IN", 128 + lo, 128 + hi), O.max)
+            tt(c("SEL", lo, hi), c("M2", lo, hi), c("INB", lo, hi), O.is_gt)
+            tt(c("SEL", lo, hi), c("SEL", lo, hi), c("D12", lo, hi), O.mult)
+            tt(c("SS", lo, hi), c("SEL", lo, hi), c("H", lo, hi), O.add)
+            cp(ind(r("FW"), c("OUR", 4 * hs, 4 * hs + 4)), c("SS", lo, hi))
+        for n, k in enumerate(order):
+            bs = [sub("XD%d" % k, "QR", 64 * blk[k][0], u) for u in range(2)]
+            if lag:
+                flush(lag.pop())
+            lag.append((k, bs, n % 2))
+        cp(r("WNF"), r("NU"))
+        tt(r("D12"), c("H", 128, 256), c("H", 0, 128), O.subtract)
+        ts(r("BS"), r("BI"), -1797120.0, O.add)
+        for k in range(2):
+            ts(r("SX%d" % k), r("GS%d" % k), 192.0, O.add)
+        if t == 0:
+            ts(c("FW", 0, 2048), r("FD"), 4095, AND); ts(c("FW", 2048, 4096), r("FD"), 12, SHR)
+        ts(r("DDM"), r("DDR"), col(10), O.mult, col(11 + t), O.add)
+        tt(r("VL"), r("A"), r("DDM"), O.add)
+        cp(ind(r("V"), r("OUR")), r("VL"))
+        tt(r("QF"), ind(r("V"), r("OU")), c("Q", 0, 256), O.add)
+        ts(c("Q", 0, 256), r("QF"), 0.5, O.mult, 95.75, O.add)
+        decide(0)
+        dup_compare("NR", "WNF")
+        flush(lag.pop())
+        dup_count()
+        decide(1)
+        cp(c("CF", 0, 256), ind(r("FW"), r("OU")))
+        if t < STEPS - 1:
+            cp(r("CU"), c("CF", 0, 256))
+
+    def disk_write(t):
+        ts(r("SI"), c("PT", 256, 384), 1797120.0, O.add)
+        cp(r("NI"), r("NU"))
+        ts(r("N1"), r("NI"), 1, AND)
+        ts(r("N1"), r("N1"), -2.0, O.mult, 1.0, O.add)
+        tt(r("NI"), r("NI"), r("N1"), O.add)
+        tt(r("MF"), c("PC", 272, 280), r("DSM"), O.mult)
+        tt(r("MF"), r("MF"), r("NI"), O.max)
+        cp(r("MU"), r("MF"))
+        if t < 3:
+            cp(ind(r("LF%d" % t), r("MU")), r("SI"))
+            send(rank + (3 if t < 2 else 2), ("LF%d" % (t + 1), 1024), c("LF%d" % t, 0, 1024), "af%d" % (t + 1))
+            if t == 2:
+                send(rank + 3, ("LFF", 1024), c("LF2", 0, 1024), "aff")
+        else:
+            cp(r("K1"), r("SI"))
+            send(rank + 1, ("SD", 128), r("K1"), "asd")
+            send(rank + 1, ("MD", 8), r("MU"), "amd")
+
+    def claims1(t):
+        dup_flag(r("FL"))
+        wrap(c("PC", 272, 280), "Z1", "FL")
+        tt(r("N12"), c("IN", 0, 128), c("IN", 128, 256), O.max)
+        ts(r("NEW"), r("N12"), -1.0, O.mult, 1.0, O.add)
+        mm(c("PC", 384, 512), r("TRI"), r("NEW"), True, True)
+        for k in range(2):
+            tags(c("PT", 256 + 64 * k, 320 + 64 * k), "GS%d" % k, "SX%d" % k)
+        ts(r("K1"), r("SS"), 1024.0, O.mult)
+        tt(r("KK"), r("K1"), r("BI"), O.add)
+        act(r("KKE"), r("KK"), F.Identity, col(20)); act(r("KKO"), r("KK"), F.Identity, col(21))
+
+    def claims2(t):
+        ts(r("PEN"), c("PC", 384, 512), -16.0, O.is_gt, B24, O.mult)
+        tt(r("KEC", A_, A_, slice(0, 16)), r("PEN"), r("KKE"), O.add)
+        tt(r("KEC", A_, A_, slice(16, 32)), r("PEN"), r("KKO"), O.add)
+        trn(r("KTC"), r("KEC"))
+        scan(r("SNC"), c("RST", 0, 256), r("KTC"), 67108864.0, O.max, O.min)
+        cp(r("KI"), stp("SNC", 31, 256, 32))
+        ts(r("PI"), r("KI"), 10, SHR)
+        ts(r("BW"), r("KI"), 1023, AND)
+        tt(r("PF"), r("PI"), r("INV"), O.max)
+        tt(r("PF"), r("PF"), r("DSC"), O.min)
+        cp(r("PU"), r("PF"))
+        cp(r("BU"), r("BW"))
+        gat("v", r("GP"), r("V"), r("PU"), 192.0)
+        gat("v", r("XP"), r("V"), r("PU"), 192.0)
+        gat("v", r("DB"), r("DIG"), r("BU"))
+        tt(r("DP"), r("GP"), r("XP"), O.subtract)
+        ts(r("ZC"), r("DP"), -(t + 1) / 16.0, O.is_equal, col(15 + t), O.mult)
+
+    def claims3(t):
+        mm(c("PR", 0, 128), r("RN"), r("DP"), True, True)
+        o = c("PT", 384, 512)
+        mm(o, r("ID"), r("XP"), True, False); mm(o, r("KEEP"), r("DP"), False, False)
+        mm(o, r("ID"), r("DB"), False, False); mm(o, r("ID"), r("ZC"), False, True)
+        cp(r("PLR"), c("PR", 0, 128))
+        dup_compare("PLR", "PF")
+        ts(r("NV"), o, -192.0, O.add)
+
+    def claims4(t):
+        dup_count()
+        dup_flag(r("FL"))
+
+    def claims5(t):
+        tt(r("FS"), c("PC", 272, 280), r("DSC"), O.mult)
+        tt(r("P2"), r("FS"), r("PF"), O.max)
+        cp(r("PU2"), r("P2"))
+        cp(ind(r("V"), r("PU2")), r("NV"))
+
+    for t in range(STEPS):
+        choice(t)
+        pick(t)
+        translate(t)
+        claims1(t)
+    disk_write(STEPS - 1)
+    dma("y", r("yc"), c("CF", 0, 256))
+    ts(r("YQ"), c("Q", 0, 256), -192.0, O.add)
+    dma("c", r("yq"), r("YQ"))
+    for n in range(5):
+        w = 32.0 * 8 ** n if n < 4 else 0.0
+        if n < 4:
+            ts(r("TI%d" % n), r("IDF"), w, O.mult); ts(r("TJ%d" % n), r("IDF"), -w, O.mult)
+    cp(c("YL", 0, 1024), c("LFF", 0, 1024))
+    claims2(STEPS - 1); claims3(STEPS - 1); claims4(STEPS - 1)
+    wrap(c("PC", 272, 280), "Z1", "FL")
+    claims5(STEPS - 1)
+    for n in range(5):
+        dma("y" if n % 2 else "c", c("TX", 256 * n, 256 * n + 256), r("V", slice(n, None, 16), slice(0, 4096)))
+    cp(ind(r("YL"), r("MD")), r("SD"))
+    dma("y", r("yl"), c("YL", 0, 1024))
+    ts(r("TD"), r("TX"), 192.0, O.add)
+    for n in range(4):
+        mm(c("PT", 0, 256), r("TI%d" % n), c("TX", 256 * n, 256 * n + 256), n == 0, False)
+        mm(c("PT", 0, 256), r("TJ%d" % n), c("TD", 256 * n, 256 * n + 256), False, n == 3)
+    ts(r("TE"), c("TX", 1024, 1280), 192.0625, O.add)
+    tt(r("TE2"), r("TE"), c("TD", 1024, 1280), O.subtract)
+    ts(r("TE2"), r("TE2"), 0.125, O.is_equal, 3594240.0, O.add)
+    tt(r("TY"), c("PT", 0, 256), r("TE2"), O.add)
+    dma("c", r("yt"), r("TY"))
+    for s in sorted(total):
+        g.wait_ge(T.sem[s], total[s])

@@ -5,7 +5,9 @@ STEPS = 4
 CHOICE = "svss"
 CL1, CL2, CU2 = 2, 3, 1
 TRANS = "vsvs"
-SUMV = 5
+CEAT = 1
+HALF = 32
+SUMV = 7
 
 
 def _scratch():
@@ -14,13 +16,14 @@ def _scratch():
     def sb(n, w, d="float32"):
         S[n] = ("sbuf", [128] + (w if isinstance(w, list) else [w]), d)
     B, I, U = "bfloat16", "int32", "uint16"
-    sb("V", 4224, B); sb("X0", 4096, B); sb("FW", 4224, I); sb("FD", 2048, I)
-    for k in range(4):
-        sb("LF%d" % k, 1280, I)
-    sb("LFF", 1280, I); sb("LFH", 1024, I); sb("YL", 1280); sb("SD", 128); sb("MD", 8, U)
+    sb("V", 4224, B); sb("FW", 4224, I); sb("FD", 2048, I)
+    for k in range(6):
+        sb("E%d" % k, 136)
+    sb("LFF", 1280, I); sb("LFH", 1024, I); sb("YL", 1280); sb("MX", 8, U)
     for k in range(3):
+        sb("LF%d" % k, 1280, I); sb("U%d" % k, 1024, U)
         sb("XL%d" % k, 1152, B)
-    sb("XLH", 1024, B)
+    sb("XLH", 1024, B); sb("HU", 1024, U)
     sb("CI", 256, I); sb("CF", 384); sb("CU", 256, U); sb("Q", 384, B); sb("CE", [16, 16]); sb("CO", [16, 16])
     for k in range(4):
         sb("XG%d" % k, 1024, B); sb("XD%d" % k, 1024, B); sb("AB%d" % k, 512, B)
@@ -38,7 +41,7 @@ def _scratch():
     sb("KI", 8, I); sb("PI", 8, I); sb("BW", 8, I); sb("BU", 8, U); sb("PF", 8); sb("PU", 8, U); sb("P2", 8); sb("PU2", 8, U)
     sb("GP", 128); sb("XP", 128, B); sb("DP", 128, B); sb("DB", 128, B); sb("ZC", 128, B); sb("NV", 128, B); sb("PLR", 128, U)
     sb("EQ2", [8, 144], B); sb("FL", 128, B); sb("FS", 8)
-    sb("VL", 128, B); sb("QF", 256); sb("SI", 128, I)
+    sb("VL", 128, B); sb("QF", 256); sb("SF", 136); sb("BA", 384, I); sb("NA", 16, U)
     sb("NI", 8, I); sb("N1", 8, I); sb("MF", 8); sb("MU", 8, U)
     sb("YQ", 256, B); sb("TX", 5 * 256, B); sb("TD", 5 * 256, B); sb("TE", 256); sb("TE2", 256); sb("TY", 256); sb("TW", 256)
     sb("COL", 64); sb("IP", 4, I); sb("BO", 128); sb("BO1", 128); sb("TF4", 80)
@@ -60,7 +63,7 @@ def _scratch():
 def _pack(S):
     real, virt, width = {}, {}, {}
     for n, (where, sh, d) in S.items():
-        if where == "psum" or len(sh) > 2 or sh[1] > 400 or n in ("SD", "MD"):
+        if where == "psum" or len(sh) > 2 or sh[1] > 400 or n in ("E0", "E1", "E2", "E3", "E4", "E5"):
             real[n] = (where, sh, d)
         else:
             unit = 8 if d in ("float32", "int32") else 16
@@ -74,7 +77,7 @@ def _pack(S):
 
 ALL = _scratch()
 SCRATCH, VIRT = _pack(ALL)
-ARR = ["ax0", "ax1", "ax2", "af0", "af1", "af2", "af3", "aff", "asd", "amd"]
+ARR = ["ax0", "ax1", "ax2", "af0", "af1", "af2", "aff"] + ["ae%d" % k for k in range(6)]
 SEMAPHORES = ["pv", "pc", "pt", "pg"] + ARR + ["d%d" % k for k in range(70)]
 PSUM = ("ps0", "ps1", "ps2", "ps3", "PA", "PT", "PR", "PC")
 MASKS = {}
@@ -116,14 +119,14 @@ def rank_program(g, core, T, topo):
     def ind(w, o):
         return (w[0].indirect(o[0]), w[1] + o[1], w[1])
 
-    def issue(q, fn, outs, ins, dma=None, rows=None):
+    def issue(q, fn, outs, ins, dma=None, rows=None, after=None):
         need = []
         rd = [x for o in ins for x in o[1]]
         wt = [x for o in outs for x in (o[2] if len(o) > 2 else o[1])]
         for o in outs:
             if len(o) > 2:
                 rd += [x for x in o[1] if x not in o[2]]
-        for n, m in rd:
+        for n, m in rd + (list(after[1]) if after else []):
             if n in PSUM:
                 continue
             for e in W.get(n, []):
@@ -179,19 +182,19 @@ def rank_program(g, core, T, topo):
                 R[n] = [e for e in R.get(n, []) if not (e[2] == mark and mark != "dma" and e[0] & ~m == 0)] + [(m, tok, mark)]
         return tok
 
-    def dma(q, out, in_, accum=False, rows=None):
+    def dma(q, out, in_, accum=False, rows=None, after=None):
         s = "d%d" % nd[0]; nd[0] += 1
         if accum:
-            issue(q, lambda: eng[q].dma_start(out[0], in_[0], accum_op=O.add, max_dma_last_dim=4096), [out], [in_, out], (s, 16, True))
+            issue(q, lambda: eng[q].dma_start(out[0], in_[0], accum_op=O.add), [out], [in_], (s, 16, True), rows)
         else:
-            issue(q, lambda: eng[q].dma_start(out[0], in_[0]), [out], [in_], (s, 16, True), rows)
+            issue(q, lambda: eng[q].dma_start(out[0], in_[0]), [out], [in_], (s, 16, True), rows, after)
 
-    def send(dst, out, in_, rsem):
+    def send(dst, out, in_, rsem, after=None):
         s = "d%d" % nd[0]; nd[0] += 1
         d = T.cores[dst % 4]
         rid, pid, _ = topo.addr(d)
         m = topo.mask(core, d)
-        issue("g", lambda: g.remote_dma(T[out[0]][:, 0:out[1]], in_[0], T.sem[rsem], T.sem[s], pid, rid, m), [], [in_], (s, len(topo.engines(core, d)), False))
+        issue("g", lambda: g.remote_dma(T[out[0]][:, 0:out[1]], in_[0], T.sem[rsem], T.sem[s], pid, rid, m), [], [in_], (s, len(topo.engines(core, d)), False), None, after)
 
     def lands(out, rsem, src):
         k = len(topo.engines(T.cores[src % 4], core))
@@ -263,23 +266,25 @@ def rank_program(g, core, T, topo):
     A_ = slice(None)
     SHR, AND = O.logical_shift_right, O.bitwise_and
 
-    dma("y", r("CI"), r("cx")); dma("c", r("TGL"), r("tg")); dma("y", r("X0"), r("xr")); dma("c", c("YQ", 0, 256), r("qx"))
+    dma("y", r("CI"), r("cx")); dma("c", r("TGL"), r("tg")); dma("y", c("V", 0, 4096), r("xr")); dma("g", c("YQ", 0, 256), r("qx"))
+    dma("y", r("XLH"), r("xl"))
 
     iota(c("IP", 0, 1), [[1, 1]], 0, 1)
     iota(r("NM"), [[1, 256]], 0, 256)
     iota(r("J16"), [[1, 16]], 0, 0, True)
     iota(r("I8"), [[16, 8]], 0, 0, True)
     ms(r("ON128"), 1.0)
-    ms(r("V"), 0.0)
+    dma("y", r("LFH"), r("lf"), after=c("V", 0, 4096))
     for j in range(4):
         ts(c("DI", (5 + j) * 256, (6 + j) * 256), r("NM"), 3 * j, SHR, 7, AND)
     ts(c("DG", 1280, 2304), c("DI", 1280, 2304), 0.0625, O.mult)
+    cp(r("CU"), r("CI"))
+    cp(c("CF", 0, 256), r("CI"))
+    ts(c("Q", 0, 256), c("YQ", 0, 256), 192.0, O.add)
     for j in range(4):
         ts(c("DI", j * 256, (j + 1) * 256), r("TGL"), 1 + 3 * j, SHR, 7, AND)
     ts(c("DI", 1024, 1280), r("TGL"), 1, AND)
     ts(c("DG", 0, 1280), c("DI", 0, 1280), 0.0625, O.mult)
-    for f in (5, 6, 7, 8, 0, 1, 2, 3, 4):
-        dma("y", r("V", slice(f, None, 16), slice(0, 4096)), c("DG", f * 256, f * 256 + 256), rows="V")
     aff(r("BO1"), r("ON128"), [[-16, 8], [0, 16]], 0, 1)
     aff(r("BO"), r("BO1"), [[16, 8], [0, 16]], 15, -1)
     aff(r("IDF"), r("ON128"), [[-1, 128]], 0, 1, O.is_equal)
@@ -288,28 +293,28 @@ def rank_program(g, core, T, topo):
     iota(r("PJ"), [[1, 8]], 0, 8)
     iota(c("CB", 0, SUMV), [[16, SUMV]], 256, 0, True)
     iota(c("CB", SUMV, 8), [[32, 8 - SUMV]], 32 * SUMV, 0, True)
-    dma("y", r("LFH"), r("lf")); dma("y", r("XLH"), r("xl")); dma("y", r("FD"), r("fd"))
-    dma("g", c("V", 0, 4096), r("xr"), True)
-    for src, b, s in ((1, "XL0", "ax0"), (2, "XL1", "ax1"), (3, "XL2", "ax2")):
+    for src, b, s in ((1, "XL0", "ax0"), (2, "XL1", "ax1"), (3, "XL2", "ax2"), (1, "U0", "af0"), (2, "U1", "af1"), (3, "U2", "af2"), (1, "LFF", "aff")):
         lands(c(b, 0, 1024), s, rank + src)
-    for src, b, s, w in ((1, "LF0", "af0", 1024), (1, "LF1", "af1", 1024), (1, "LF2", "af2", 1024), (2, "LF3", "af3", 1024), (1, "LFF", "aff", 1024), (3, "SD", "asd", 128), (3, "MD", "amd", 8)):
-        lands(c(b, 0, w), s, rank + src)
-    send(rank + 3, ("LF0", 1024), r("LFH"), "af0")
+    for k, src in enumerate((1, 2, 1, 3, 2, 3)):
+        lands(r("E%d" % k), "ae%d" % k, rank + src)
+    iota(c("Q", 256, 384), [[0, 128]], 192, 0, True); iota(c("CF", 256, 384), [[0, 128]], 0, 0, True)
+    for k in range(3):
+        iota(c("LF%d" % k, 1024, 1152), [[0, 128]], 0, 0)
+        iota(c("XL%d" % k, 1024, 1152), [[0, 128]], 0, 0, True)
+    iota(c("DD", 256, 384), [[0, 128]], 0, 0, True)
+    iota(c("BA", 256, 384), [[0, 128]], 0, 0)
+    iota(r("DIG"), [[0, 1024]], 0, 0, True)
     send(rank + 3, ("XL0", 1024), r("XLH"), "ax0")
-    send(rank + 2, ("XL1", 1024), r("XLH"), "ax1")
-    send(rank + 1, ("XL2", 1024), r("XLH"), "ax2")
-    cp(r("CU"), r("CI"))
-    cp(c("CF", 0, 256), r("CI"))
-    ts(c("Q", 0, 256), c("YQ", 0, 256), 192.0, O.add)
-    ms(c("Q", 256, 384), 192.0); ms(c("CF", 256, 384), 0.0)
-    ts(c("IP", 1, 2), c("IP", 0, 1), 15, AND)
-    ts(c("IP", 2, 3), c("IP", 0, 1), 4, SHR, 1, AND)
-    cp(col(0), c("IP", 1, 2)); cp(col(1), c("IP", 2, 3))
+
+    def digits():
+        for f in (5, 6, 7, 8, 0, 1, 2, 3, 4):
+            dma("g", r("V", slice(f, None, 16), slice(0, 4096)), c("DG", f * 256, f * 256 + 256), True, rows="V")
+            if f == 0:
+                cp(r("HU"), r("LFH"))
+                send(rank + 3, ("U0", 1024), r("HU"), "af0")
+        send(rank + 2, ("U1", 1024), r("HU"), "af1", r("U0"))
+        send(rank + 2, ("XL1", 1024), r("XLH"), "ax1")
     B24 = 16777216.0
-    ts(col(20), col(1), B24, O.mult)
-    ts(col(21), col(1), -B24, O.mult, B24, O.add)
-    ts(col(24), col(0), 4096.0, O.mult)
-    tt(col(2), col(24), col(20), O.add); tt(col(3), col(24), col(21), O.add)
 
     def total_of(o, a, b):
         tmp = c("TF4", 32, 32 + int(a[0].shape[1]))
@@ -324,12 +329,21 @@ def rank_program(g, core, T, topo):
 
     def zbuf(n, w):
         scaled(stp(n, 15, 143, 16), stp("BO", 0, 128, 16), w)
-    for n in ("ZK", "ZKN", "ZT", "ZTN", "ZN", "Z1"):
-        ms(r(n), 0.0)
+    ms(r("ZK"), 0.0)
     scaled(r("ID"), r("IDF"), 1.0); scaled(r("NID"), r("IDF"), -1.0)
     zbuf("ZK", 65536)
 
     def consts():
+        ts(c("IP", 1, 2), c("IP", 0, 1), 15, AND)
+        ts(c("IP", 2, 3), c("IP", 0, 1), 4, SHR, 1, AND)
+        cp(col(0), c("IP", 1, 2)); cp(col(1), c("IP", 2, 3))
+        ts(col(20), col(1), B24, O.mult)
+        ts(col(21), col(1), -B24, O.mult, B24, O.add)
+        ts(col(24), col(0), 4096.0, O.mult)
+        tt(col(2), col(24), col(20), O.add); tt(col(3), col(24), col(21), O.add)
+        act(r("CE"), c("CF", 0, 256), F.Identity, col(2)); act(r("CO"), c("CF", 0, 256), F.Identity, col(3))
+        for n in ("ZKN", "ZT", "ZTN", "ZN", "Z1"):
+            ms(r(n), 0.0)
         ts(c("TF4", 0, 16), r("J16"), col(0), O.is_equal)
         ms(c("TF4", 16, 32), 0.5); ms(c("TF4", 64, 80), 0.0)
         scan(c("POW", 0, 16), c("TF4", 16, 32), c("TF4", 64, 80), 65536.0, O.mult, O.add)
@@ -342,11 +356,11 @@ def rank_program(g, core, T, topo):
         ts(c("COL", 15, 19), c("J16", 2, 6), c("TF4", 4, 5), O.mult, -0.0625, O.mult)
         ts(col(19), col(4), -1.0, O.mult)
         ms(r("RST"), 0.0); ms(stp("RST", 0, 512, 32), 67108864.0)
+        digits()
         zbuf("ZN", col(5)); zbuf("ZT", col(4)); zbuf("ZTN", col(19)); zbuf("ZKN", -65536); zbuf("Z1", 0.0625)
         for n, w in (("RN", col(5)), ("RE", col(6)), ("RL128", col(4)), ("RD", col(7)), ("RB", 65536.0)):
             scaled(r(n), r("BO"), w)
         scaled(r("KEEP"), r("IDF"), col(9)); scaled(r("K1"), r("IDF"), -16.0)
-        tt(r("TRI"), r("LTF"), r("K1"), O.add)
         ts(c("CT2", 0, 16), c("POW", 0, 16), 2.0, O.mult)
         for k in (16, 32, 64, 128):
             cp(c("CT2", k, 2 * k), c("CT2", 0, k))
@@ -356,27 +370,27 @@ def rank_program(g, core, T, topo):
         ts(r("SW8"), r("I8"), col(0), O.add); ts(r("SC8"), r("SW8"), 0.5, O.add); ts(r("SW2"), r("SW8"), 2.0, O.mult)
         ts(r("DSC"), r("SW8"), 4096.0, O.add); ts(r("DSM"), r("SW8"), 1152.0, O.add)
         ms(r("ONE"), 1.0)
+
+    def pads():
         for j in range(3):
             ts(c("PJD", 8 * j, 8 * j + 8), r("PJ"), 3 * j, SHR, 7 if j < 2 else 1, AND)
         ts(c("PD", 0, 24), r("PJD"), 0.0625, O.mult)
         ms(c("PD", 24, 32), 0.125); ms(c("PD", 32, 40), 0.5)
-        ms(c("DD", 256, 384), 0.0)
         for f, k in ((0, 0), (1, 1), (2, 2), (3, 3), (5, 0), (6, 1), (7, 2), (8, 4)):
             dma("y", r("DD", slice(f, None, 16), slice(256, 384)), c("PD", 8 * k, 8 * k + 8), rows="DD")
-        for k in range(4):
-            ms(c("LF%d" % k, 1024, 1280), 0)
-        for k in range(3):
-            ms(c("XL%d" % k, 1024, 1152), 0.0)
+
+    def labels():
         ts(r("NB"), r("NB"), 1023, AND)
         for j in range(4):
             ts(c("NBD", 64 * j, 64 * j + 64), r("NB"), 3 * j, SHR, 7, AND)
         ts(c("NBB", 0, 256), r("NBD"), 0.0625, O.mult)
         ms(c("NBB", 256, 320), 0.0625)
-        ms(r("DIG"), 0.0)
         for f in range(5):
             dma("y", r("DIG", slice(f, None, 16)), c("NBB", 64 * f, 64 * f + 64), rows="DIG")
         act(c("V", 4096, 4224), c("DD", 256, 384))
-        ms(c("FW", 4096, 4224), 0)
+        tt(r("TRI"), r("LTF"), r("K1"), O.add)
+        for n in range(4):
+            scaled(r("TI%d" % n), r("IDF"), 32.0 * 8 ** n); scaled(r("TJ%d" % n), r("IDF"), -32.0 * 8 ** n)
 
     pk = [0]
 
@@ -418,24 +432,29 @@ def rank_program(g, core, T, topo):
             mm(o, sel(z, a), stp(x, a, 128, 16), a == 0, a == 15)
 
     def choice(t):
-        win = r("X0") if t == 0 else c("V", 0, 4096)
+        win = c("V", 0, 4096)
 
-        def take(k):
-            gat("v" if CHOICE[k] == "v" else "c", r("XG%d" % k), win, c("CU", 64 * k, 64 * k + 64), 192.0)
+        def take(k, a=0, b=64):
+            gat("v" if CHOICE[k] == "v" or k == late and a == 0 else "c", c("XG%d" % k, 16 * a, 16 * b), win, c("CU", 64 * k + a, 64 * k + b), 192.0)
         order = [k for k in range(4) if CHOICE[k] == "v"] + [k for k in range(4) if CHOICE[k] != "v"]
-        late = order[-1] if CHOICE.count("v") < 3 else None
+        late = order[-1]
         for k in order:
             if k != late:
                 take(k)
+        half = HALF if t else 64
+        take(late, 0, half)
         if t:
+            claims1(t - 1)
             disk_write(t - 1)
             claims2(t - 1)
         lag = None
         for n, k in enumerate(order):
             for u in range(2):
                 b = sub("XG%d" % k, "Q", 64 * k, u)
-                if n == 0 and u == 1 and late is not None:
-                    take(late)
+                if n == 0 and u == 1 and half < 64:
+                    take(late, half)
+                if t and n == CEAT and u == 1:
+                    act(r("CE"), c("CF", 0, 256), F.Identity, col(2)); act(r("CO"), c("CF", 0, 256), F.Identity, col(3))
                 if lag:
                     sums(*lag)
                 lag = (b, "ZK", c("PA", 64 * k, 64 * k + 64), u, True, True)
@@ -443,7 +462,6 @@ def rank_program(g, core, T, topo):
                     claims4(t - 1)
             if t and n == CL1:
                 claims3(t - 1)
-        act(r("CE"), c("CF", 0, 256), F.Identity, col(2)); act(r("CO"), c("CF", 0, 256), F.Identity, col(3))
         sums(*lag)
         if t == 0:
             consts()
@@ -462,11 +480,16 @@ def rank_program(g, core, T, topo):
         cp(r("OF"), r("OI"))
         if t:
             claims5(t - 1)
-        gat("c", r("VO"), r("V"), r("OU"), 192.0)
-        gat("v", r("XO"), r("V"), r("OU"), 192.0)
+        else:
+            pads()
+            dma("y", r("FD"), r("fd"), after=c("V", 0, 4096))
+        gat("c", r("VO"), c("V", 0, 4096), r("OU"), 192.0)
+        gat("v", r("XO"), c("V", 0, 4096), r("OU"), 192.0)
         tt(c("DD", 0, 256), r("VO"), r("XO"), O.subtract)
         mm(c("PR", 0, 256), r("RN"), c("DD", 0, 256), True, True)
         mm(c("PC", 0, 256), r("RE"), c("DD", 0, 256), True, False)
+        for a in range(16):
+            mm(c("PT", 0, 16), sel("ZT", a), stp("DD", a, 256, 16), a == 0, a == 15)
         cp(r("OR"), c("PR", 0, 256))
         for b in range(16):
             ts(r("EQ", A_, b, slice(0, 256 - 16 * b)), c("OR", 16 * b, 256), c("OF", b, b + 1), O.is_equal)
@@ -485,21 +508,26 @@ def rank_program(g, core, T, topo):
         ts(r("RL"), r("SW2"), r("T2"), O.subtract, 0.0, O.max)
         tt(r("CBP"), r("CB"), r("RL"), O.add)
         ts(r("INV"), r("SW2"), r("T2"), O.is_ge, 8192.0, O.mult)
+        if t:
+            apply(2 * (t - 1), "LF%d" % (t % 3))
+        else:
+            cp(c("LF0", 0, 1024), r("U0"))
+        cp(r("NA"), c("PT", 0, 16))
+        gat("v", c("BA", 0, 256), c("LF%d" % (t % 3), 0, 1152), r("NA"))
         tt(r("H8"), r("LS"), r("CBP"), O.add)
         ts(r("LU"), r("H8"), 0.5, O.mult)
-        gat("v", r("DDR"), r("DD"), r("LU"))
+        gat("v", r("BI"), r("BA"), r("LU"))
         gat("c", r("CR"), r("CF"), r("LU"))
         gat("c", r("QR"), r("Q"), r("LU"))
+        tt(r("SQ"), r("BI"), r("BI"), O.mult)
+        cp(r("CRU"), r("CR"))
+        gat("v", r("DDR"), r("DD"), r("LU"))
         wrap(c("PR", 256, 264), "ZT", "DDR")
 
     def translate(t):
-        LF, XL = "LF%d" % t, "XL%d" % (t % 3)
-        cp(r("NU"), c("PR", 256, 264))
+        LF, XL = "LF%d" % (t % 3), "XL%d" % (t % 3)
         wrap(c("PC", 264, 272), "ZN", "DDR")
         mm(c("PC", 0, 128), r("RL128"), r("DDR"), True, True)
-        gat("v", r("BI"), r(LF, A_, slice(0, 1152)), r("NU"))
-        tt(r("SQ"), r("BI"), r("BI"), O.mult)
-        cp(r("CRU"), r("CR"))
         ts(c("H", 0, 128), r("SQ"), 3, SHR)
         ts(r("S5"), r("SQ"), 5, SHR)
         ts(c("H", 128, 256), r("BI"), 37.0, O.mult, 1.0, O.add)
@@ -508,24 +536,18 @@ def rank_program(g, core, T, topo):
         ts(r("H"), r("H"), 4095, AND)
         cp(r("CCU"), r("H"))
         for k in range(2):
-            gat("c", r("GS%d" % k), r("V"), c("CRU", 64 * k, 64 * k + 64))
+            gat("c", r("GS%d" % k), c("V", 0, 4096), c("CRU", 64 * k, 64 * k + 64))
         blk = [(0, 0), (0, 1), (1, 0), (1, 1)]
-        done = []
-        for k, (hs, w) in enumerate(blk):
-            lo = 128 * w + 64 * hs
-            gat("v" if TRANS[k] == "v" else "c", r("XG%d" % k), r("V"), c("CCU", lo, lo + 64))
-            dec = [j for j in range(k + 1) if j not in done and (TRANS[j] == "v" or k > j or k == 3)]
-            for j in dec:
-                ts(r("XD%d" % j), r("XG%d" % j), 192.0, O.add)
-                done.append(j)
-            if k == 0:
-                cp(r("OUR"), c("PC", 264, 272))
-                cp(r("NR"), c("PC", 0, 128))
-        gat("c", r("A"), r(XL), r("NU"))
-        lag = []
-        order = [k for k in range(4) if TRANS[k] == "v" and blk[k][0] == 0] + [k for k in range(4) if TRANS[k] != "v" and blk[k][0] == 0]
-        order += [k for k in range(4) if TRANS[k] == "v" and blk[k][0] == 1] + [k for k in range(4) if TRANS[k] != "v" and blk[k][0] == 1]
 
+        def take(k):
+            lo = 128 * blk[k][1] + 64 * blk[k][0]
+            gat("v" if TRANS[k] == "v" else "c", r("XG%d" % k), c("V", 0, 4096), c("CCU", lo, lo + 64))
+
+        def plain(k):
+            ts(r("XD%d" % k), r("XG%d" % k), 192.0, O.add)
+
+        def subs(k):
+            return [sub("XD%d" % k, "QR", 64 * blk[k][0], u) for u in range(2)]
         bank = [("PC", 128, "PR", 384), ("PT", 0, "PA", 256)]
 
         def flush(x):
@@ -546,62 +568,98 @@ def rank_program(g, core, T, topo):
             tt(c("SEL", lo, hi), c("M2", lo, hi), c("INB", lo, hi), O.is_gt)
             tt(c("SEL", lo, hi), c("SEL", lo, hi), c("D12", lo, hi), O.mult)
             tt(c("SS", lo, hi), c("SEL", lo, hi), c("H", lo, hi), O.add)
+            if hs == 0:
+                claim_keys(lo, hi)
             cp(ind(r("FW"), c("OUR", 4 * hs, 4 * hs + 4)), c("SS", lo, hi))
-        for n, k in enumerate(order):
-            bs = [sub("XD%d" % k, "QR", 64 * blk[k][0], u) for u in range(2)]
-            if lag:
-                flush(lag.pop())
-            lag.append((k, bs, n % 2))
+        take(0); plain(0)
+        cp(r("NU"), c("PR", 256, 264))
+        cp(r("OUR"), c("PC", 264, 272))
+        cp(r("NR"), c("PC", 0, 128))
+        take(1)
+        b0 = subs(0)
+        plain(1)
+        take(2); take(3)
+        b1 = subs(1)
+        gat("c", r("A"), r(XL), r("NU"))
+        flush((0, b0, 0))
+        plain(2)
+        b2 = subs(2)
+        flush((1, b1, 1))
+        plain(3)
+        lag = [(3, subs(3), 1)]
+        flush((2, b2, 0))
         cp(r("WNF"), r("NU"))
         tt(r("D12"), c("H", 128, 256), c("H", 0, 128), O.subtract)
         ts(r("BS"), r("BI"), -1797120.0, O.add)
         for k in range(2):
             ts(r("SX%d" % k), r("GS%d" % k), 192.0, O.add)
         if t == 0:
-            ts(c("FW", 0, 2048), r("FD"), 4095, AND); ts(c("FW", 2048, 4096), r("FD"), 12, SHR)
+            labels()
+            ts(c("FW", 0, 2048), r("FD"), 4095, AND)
+            ts(c("FW", 2048, 4096), r("FD"), 12, SHR)
         ts(r("DDM"), r("DDR"), col(10), O.mult, col(11 + t), O.add)
         tt(r("VL"), r("A"), r("DDM"), O.add)
         cp(ind(r("V"), r("OUR")), r("VL"))
-        tt(r("QF"), ind(r("V"), r("OU")), c("Q", 0, 256), O.add)
+        tt(r("QF"), ind(c("V", 0, 4096), r("OU")), c("Q", 0, 256), O.add)
         ts(c("Q", 0, 256), r("QF"), 0.5, O.mult, 95.75, O.add)
-        decide(0)
-        dup_compare("NR", "WNF")
-        flush(lag.pop())
-        dup_count()
-        decide(1)
-        cp(c("CF", 0, 256), ind(r("FW"), r("OU")))
-        if t < STEPS - 1:
-            cp(r("CU"), c("CF", 0, 256))
-
-    def disk_write(t):
-        ts(r("SI"), c("PT", 256, 384), 1797120.0, O.add)
         cp(r("NI"), r("NU"))
         ts(r("N1"), r("NI"), 1, AND)
         ts(r("N1"), r("N1"), -2.0, O.mult, 1.0, O.add)
         tt(r("NI"), r("NI"), r("N1"), O.add)
-        tt(r("MF"), c("PC", 272, 280), r("DSM"), O.mult)
-        tt(r("MF"), r("MF"), r("NI"), O.max)
-        cp(r("MU"), r("MF"))
-        if t < 3:
-            cp(ind(r("LF%d" % t), r("MU")), r("SI"))
-            send(rank + (3 if t < 2 else 2), ("LF%d" % (t + 1), 1024), c("LF%d" % t, 0, 1024), "af%d" % (t + 1))
-            if t == 2:
-                send(rank + 3, ("LFF", 1024), c("LF2", 0, 1024), "aff")
-        else:
-            cp(r("K1"), r("SI"))
-            send(rank + 1, ("SD", 128), r("K1"), "asd")
-            send(rank + 1, ("MD", 8), r("MU"), "amd")
-
-    def claims1(t):
-        dup_flag(r("FL"))
-        wrap(c("PC", 272, 280), "Z1", "FL")
-        tt(r("N12"), c("IN", 0, 128), c("IN", 128, 256), O.max)
-        ts(r("NEW"), r("N12"), -1.0, O.mult, 1.0, O.add)
-        mm(c("PC", 384, 512), r("TRI"), r("NEW"), True, True)
+        decide(0)
+        if t == 1:
+            cp(c("LF2", 0, 1024), r("U2"))
+            apply(1, "LF2")
+        if t == 2:
+            apply(3, "LF0")
+        dup_compare("NR", "WNF")
+        flush(lag.pop())
+        dup_count()
+        decide(1)
+        if t == STEPS - 1:
+            dup_flag(r("FL"))
+            wrap(c("PC", 272, 280), "Z1", "FL")
+            claim_order()
         for k in range(2):
             tags(c("PT", 256 + 64 * k, 320 + 64 * k), "GS%d" % k, "SX%d" % k)
-        ts(r("K1"), r("SS"), 1024.0, O.mult)
-        tt(r("KK"), r("K1"), r("BI"), O.add)
+        cp(c("CF", 0, 256), ind(c("FW", 0, 4096), r("OU")))
+        if t < STEPS - 1:
+            cp(r("CU"), c("CF", 0, 256))
+
+    def claim_keys(lo, hi):
+        tt(c("N12", lo, hi), c("IN", lo, hi), c("IN", 128 + lo, 128 + hi), O.max)
+        ts(c("NEW", lo, hi), c("N12", lo, hi), -1.0, O.mult, 1.0, O.add)
+        ts(c("K1", lo, hi), c("SS", lo, hi), 1024.0, O.mult)
+        tt(c("KK", lo, hi), c("K1", lo, hi), c("BI", lo, hi), O.add)
+
+    def disk_write(t):
+        act(c("SF", 0, 128), c("PT", 256, 384), F.Identity, 1797120.0)
+        tt(r("MF"), c("PC", 272, 280), r("DSM"), O.mult)
+        tt(c("SF", 128, 136), r("MF"), r("NI"), O.max)
+        for dst, k in (((3, 0), (2, 1)), ((3, 2), (1, 3)), ((2, 4),), ((1, 5),))[t]:
+            send(rank + dst, ("E%d" % k, 136), r("SF"), "ae%d" % k)
+        if t == 0:
+            send(rank + 1, ("U2", 1024), r("HU"), "af2")
+            send(rank + 1, ("XL2", 1024), r("XLH"), "ax2")
+        if t in (0, 2):
+            cp(r("MU"), c("SF", 128, 136))
+            cp(ind(r("LF%d" % t), r("MU")), c("SF", 0, 128))
+        if t == 2:
+            send(rank + 3, ("LFF", 1024), c("LF2", 0, 1024), "aff")
+
+    def apply(k, n):
+        cp(r("MX"), c("E%d" % k, 128, 136))
+        cp(ind(r(n), r("MX")), c("E%d" % k, 0, 128))
+
+    def claims1(t):
+        if t < STEPS - 1:
+            dup_flag(r("FL"))
+            wrap(c("PC", 272, 280), "Z1", "FL")
+            claim_order()
+
+    def claim_order():
+        claim_keys(64, 128)
+        mm(c("PC", 384, 512), r("TRI"), r("NEW"), True, True)
         act(r("KKE"), r("KK"), F.Identity, col(20)); act(r("KKO"), r("KK"), F.Identity, col(21))
 
     def claims2(t):
@@ -628,6 +686,8 @@ def rank_program(g, core, T, topo):
         o = c("PT", 384, 512)
         mm(o, r("ID"), r("XP"), True, False); mm(o, r("KEEP"), r("DP"), False, False)
         mm(o, r("ID"), r("DB"), False, False); mm(o, r("ID"), r("ZC"), False, True)
+        if t == 0:
+            cp(c("LF1", 0, 1024), r("U1"))
         cp(r("PLR"), c("PR", 0, 128))
         dup_compare("PLR", "PF")
         ts(r("NV"), o, -192.0, O.add)
@@ -646,28 +706,25 @@ def rank_program(g, core, T, topo):
         choice(t)
         pick(t)
         translate(t)
-        claims1(t)
-    disk_write(STEPS - 1)
+    claims1(STEPS - 1)
     dma("y", r("yc"), c("CF", 0, 256))
+    disk_write(STEPS - 1)
+    claims2(STEPS - 1)
     ts(r("YQ"), c("Q", 0, 256), -192.0, O.add)
-    dma("c", r("yq"), r("YQ"))
-    for n in range(5):
-        w = 32.0 * 8 ** n if n < 4 else 0.0
-        if n < 4:
-            ts(r("TI%d" % n), r("IDF"), w, O.mult); ts(r("TJ%d" % n), r("IDF"), -w, O.mult)
-    cp(c("YL", 0, 1024), c("LFF", 0, 1024))
-    claims2(STEPS - 1); claims3(STEPS - 1); claims4(STEPS - 1)
+    dma("y", r("yq"), r("YQ"))
+    claims3(STEPS - 1); claims4(STEPS - 1)
     wrap(c("PC", 272, 280), "Z1", "FL")
     claims5(STEPS - 1)
     for n in range(5):
         dma("y" if n % 2 else "c", c("TX", 256 * n, 256 * n + 256), r("V", slice(n, None, 16), slice(0, 4096)))
-    cp(ind(r("YL"), r("MD")), r("SD"))
+    cp(c("YL", 0, 1024), c("LFF", 0, 1024))
+    apply(5, "YL")
     dma("y", r("yl"), c("YL", 0, 1024))
     ts(r("TD"), r("TX"), 192.0, O.add)
     for n in range(4):
         mm(c("PT", 0, 256), r("TI%d" % n), c("TX", 256 * n, 256 * n + 256), n == 0, False)
         mm(c("PT", 0, 256), r("TJ%d" % n), c("TD", 256 * n, 256 * n + 256), False, n == 3)
-    ts(r("TE"), c("TX", 1024, 1280), 192.0625, O.add)
+    act(r("TE"), c("TX", 1024, 1280), F.Identity, 192.0625)
     tt(r("TE2"), r("TE"), c("TD", 1024, 1280), O.subtract)
     ts(r("TE2"), r("TE2"), 0.125, O.is_equal, 3594240.0, O.add)
     tt(r("TY"), c("PT", 0, 256), r("TE2"), O.add)

import numpy as np
from concourse.mybir import AluOpType as O, AxisListType, ActivationFunctionType as F

STEPS = 4
CHOICE = "svss"
CL1, CL2, CU2 = 2, 3, 1
TRANS = "vsvs"
CEAT = 1
HALF = 32
SUMV = 7


def _scratch():
    S = {}

    def sb(n, w, d="float32"):
        S[n] = ("sbuf", [128] + (w if isinstance(w, list) else [w]), d)
    B, I, U = "bfloat16", "int32", "uint16"
    sb("V", 4224, B); sb("FW", 4224, I); sb("FD", 2048, I)
    for k in range(6):
        sb("E%d" % k, 136)
    sb("LFF", 1280, I); sb("LFH", 1024, I); sb("YL", 1280); sb("MX", 8, U)
    for k in range(3):
        sb("LF%d" % k, 1280, I); sb("U%d" % k, 1024, U)
        sb("XL%d" % k, 1152, B)
    sb("XLH", 1024, B); sb("HU", 1024, U)
    sb("CI", 256, I); sb("CF", 384); sb("CU", 256, U); sb("Q", 384, B); sb("CE", [16, 16]); sb("CO", [16, 16])
    for k in range(4):
        sb("XG%d" % k, 1024, B); sb("XD%d" % k, 1024, B); sb("AB%d" % k, 512, B)
    for k in range(2):
        sb("GS%d" % k, 1024, B); sb("SX%d" % k, 1024, B)
    sb("KEY", [16, 32]); sb("KT", 512); sb("SCN", 512); sb("RST", 512)
    sb("OI", 16, I); sb("OF", 16); sb("OU", 16, U)
    sb("VO", 256); sb("XO", 256, B); sb("DD", 384, B); sb("OR", 256, U); sb("EQ", [16, 272], B); sb("CA", 256); sb("PX", 256)
    sb("ONE", 256); sb("JS", 256, B); sb("JV", 256, B); sb("LS", 8); sb("T2", 1); sb("RL", 8); sb("CBP", 8); sb("INV", 8); sb("H8", 8); sb("LU", 8, U)
    sb("DDR", 128, B); sb("CR", 128); sb("CRU", 128, U); sb("QR", 128, B)
    sb("WNF", 8); sb("NU", 8, U); sb("OUR", 8, U); sb("NR", 128, U); sb("A", 128, B); sb("BI", 128, I); sb("BS", 128)
    sb("SQ", 128, I); sb("S5", 128, I); sb("H", 256, I); sb("CCU", 256, U); sb("D12", 128)
    sb("IN", 256, B); sb("INB", 128); sb("M2", 128); sb("SEL", 128); sb("SS", 128, I); sb("N12", 128, B); sb("NEW", 128, B)
    sb("K1", 128); sb("KK", 128); sb("KKE", [8, 16]); sb("KKO", [8, 16]); sb("PEN", [8, 16]); sb("KEC", [8, 32]); sb("KTC", 256); sb("SNC", 256)
    sb("KI", 8, I); sb("PI", 8, I); sb("BW", 8, I); sb("BU", 8, U); sb("PF", 8); sb("PU", 8, U); sb("P2", 8); sb("PU2", 8, U)
    sb("GP", 128); sb("XP", 128, B); sb("DP", 128, B); sb("DB", 128, B); sb("ZC", 128, B); sb("NV", 128, B); sb("PLR", 128, U)
    sb("EQ2", [8, 144], B); sb("FL", 128, B); sb("FS", 8)
    sb("VL", 128, B); sb("QF", 256); sb("SF", 136); sb("BA", 384, I); sb("NA", 16, U)
    sb("NI", 8, I); sb("N1", 8, I); sb("MF", 8); sb("MU", 8, U)
    sb("YQ", 256, B); sb("TX", 5 * 256, B); sb("TD", 5 * 256, B); sb("TE", 256); sb("TE2", 256); sb("TY", 256); sb("TW", 256)
    sb("COL", 64); sb("IP", 4, I); sb("BO", 128); sb("BO1", 128); sb("TF4", 80)
    for n in ("ZK", "ZKN", "ZT", "ZTN", "ZN", "Z1"):
        sb(n, 144, B)
    for n in ("ID", "NID", "RN", "RE", "RL128", "RD", "RB", "KEEP", "TRI"):
        sb(n, 128, B)
    for n in range(5):
        sb("TI%d" % n, 128, B); sb("TJ%d" % n, 128, B)
    sb("ON128", 128); sb("IDF", 128); sb("LTF", 128); sb("J16", 16); sb("POW", 20); sb("DDM", 128, B); sb("CT", 256); sb("CT2", 256)
    sb("SC8", 8); sb("SW8", 8); sb("SW2", 8); sb("DSC", 8); sb("DSM", 8); sb("CB", 8); sb("I8", 8)
    sb("TGL", 256, I); sb("NM", 256, I); sb("DI", 9 * 256, I); sb("DG", 9 * 256, B)
    sb("NB", 64, I); sb("NBD", 256, I); sb("NBB", 320, B); sb("DIG", 1024, B); sb("PJ", 8, I); sb("PJD", 24, I); sb("PD", 40, B)
    for n in ("ps0", "ps1", "ps2", "ps3", "PA", "PT", "PR", "PC"):
        S[n] = ("psum", [128, 512], "float32")
    return S


def _pack(S):
    real, virt, width = {}, {}, {}
    for n, (where, sh, d) in S.items():
        if where == "psum" or len(sh) > 2 or sh[1] > 400 or n in ("E0", "E1", "E2", "E3", "E4", "E5"):
            real[n] = (where, sh, d)
        else:
            unit = 8 if d in ("float32", "int32") else 16
            at = width.get(d, 0)
            virt[n] = ("W" + d, at, sh[1])
            width[d] = at + -(-sh[1] // unit) * unit
    for d, w in width.items():
        real["W" + d] = ("sbuf", [128, w], d)
    return real, virt


ALL = _scratch()
SCRATCH, VIRT = _pack(ALL)
ARR = ["ax0", "ax1", "ax2", "af0", "af1", "af2", "aff"] + ["ae%d" % k for k in range(6)]
SEMAPHORES = ["pv", "pc", "pt", "pg"] + ARR + ["d%d" % k for k in range(70)]
PSUM = ("ps0", "ps1", "ps2", "ps3", "PA", "PT", "PR", "PC")
MASKS = {}


def rank_program(g, core, T, topo):
    rank = T.rank_of(core)
    if rank is None:
        return
    eng = {"v": g.vector, "c": g.scalar, "t": g.tensor, "g": g, "y": g.sync}
    psem = {"v": "pv", "c": "pc", "t": "pt", "g": "pg"}
    cnt = {"v": 0, "c": 0, "t": 0, "g": 0}
    know = {q: {} for q in eng}
    W, R, X = {}, {}, {}
    total = {}
    nd = [0]

    def r(name, *idx):
        key = (name, str(idx))
        if key not in MASKS:
            if name in ALL and ALL[name][0] == "sbuf":
                sh = ALL[name][1][1:]
                n = int(np.prod(sh)); f = np.zeros(n, np.uint8)
                f[np.arange(n).reshape(sh)[tuple(idx[1:])].reshape(-1)] = 1
                MASKS[key] = int.from_bytes(np.packbits(f, bitorder="little").tobytes(), "little")
            else:
                MASKS[key] = 1
        if name in VIRT:
            arena, at, w = VIRT[name]
            cs = idx[1] if len(idx) > 1 else slice(0, w)
            lo, hi, st = cs.indices(w)
            return (T[arena][idx[0] if idx else slice(None), at + lo:at + hi:st], ((name, MASKS[key]),))
        t = T[name]
        return (t[idx] if idx else t[:], ((name, MASKS[key]),))

    def c(name, a, b):
        return r(name, slice(None), slice(a, b))

    def ind(w, o):
        return (w[0].indirect(o[0]), w[1] + o[1], w[1])

    def issue(q, fn, outs, ins, dma=None, rows=None, after=None):
        need = []
        rd = [x for o in ins for x in o[1]]
        wt = [x for o in outs for x in (o[2] if len(o) > 2 else o[1])]
        for o in outs:
            if len(o) > 2:
                rd += [x for x in o[1] if x not in o[2]]
        for n, m in rd + (list(after[1]) if after else []):
            if n in PSUM:
                continue
            for e in W.get(n, []):
                if e[0] & m:
                    need.append(e[1])
        for n, m in wt:
            if n in PSUM:
                continue
            for e in W.get(n, []):
                if e[0] & m and not (rows and e[2] == rows):
                    need.append(e[1])
            for e in R.get(n, []):
                if e[0] & m:
                    need.append(e[1])
        for n, m in rd + wt:
            if n in PSUM:
                need += [tk for q2, tk in X.get(n, {}).items() if q2 != q]
        best = {}
        for s, v, sn in need:
            if s not in best or best[s][0] < v:
                best[s] = (v, sn)
        order = sorted(best.items(), key=lambda z: -len(z[1][1]))
        for s, (v, sn) in order:
            if know[q].get(s, 0) >= v:
                continue
            if any(s2 != s and sn2.get(s, 0) >= v and know[q].get(s2, 0) < v2 for s2, (v2, sn2) in order):
                continue
            eng[q].wait_ge(T.sem[s], v)
            know[q][s] = max(know[q].get(s, 0), v)
            for a, b in sn.items():
                if know[q].get(a, 0) < b:
                    know[q][a] = b
        inst = fn()
        if dma is None:
            cnt[q] += 1
            tok = (psem[q], cnt[q], dict(know[q]))
            inst.then_inc(T.sem[psem[q]], 1)
            total[psem[q]] = cnt[q]
            mark = q
        else:
            tok = (dma[0], dma[1], dict(know[q])); total[dma[0]] = dma[1]; mark = "dma"
            if dma[2]:
                inst.then_inc(T.sem[dma[0]], 16)
        for n, m in rd + wt:
            if n in PSUM:
                X.setdefault(n, {})[q] = tok
        for n, m in wt:
            if n not in PSUM:
                W[n] = [(e[0] & ~m, e[1], e[2]) if not (rows and e[2] == rows) else e for e in W.get(n, []) if e[0] & ~m or (rows and e[2] == rows)] + [(m, tok, rows)]
                R[n] = [(e[0] & ~m, e[1], e[2]) for e in R.get(n, []) if e[0] & ~m]
        for n, m in rd:
            if n not in PSUM:
                R[n] = [e for e in R.get(n, []) if not (e[2] == mark and mark != "dma" and e[0] & ~m == 0)] + [(m, tok, mark)]
        return tok

    def dma(q, out, in_, accum=False, rows=None, after=None):
        s = "d%d" % nd[0]; nd[0] += 1
        if accum:
            issue(q, lambda: eng[q].dma_start(out[0], in_[0], accum_op=O.add), [out], [in_], (s, 16, True), rows)
        else:
            issue(q, lambda: eng[q].dma_start(out[0], in_[0]), [out], [in_], (s, 16, True), rows, after)

    def send(dst, out, in_, rsem, after=None):
        s = "d%d" % nd[0]; nd[0] += 1
        d = T.cores[dst % 4]
        rid, pid, _ = topo.addr(d)
        m = topo.mask(core, d)
        issue("g", lambda: g.remote_dma(T[out[0]][:, 0:out[1]], in_[0], T.sem[rsem], T.sem[s], pid, rid, m), [], [in_], (s, len(topo.engines(core, d)), False), None, after)

    def lands(out, rsem, src):
        k = len(topo.engines(T.cores[src % 4], core))
        total[rsem] = k
        n, m = out[1][0]
        W[n] = [(e[0] & ~m, e[1], e[2]) for e in W.get(n, []) if e[0] & ~m] + [(m, (rsem, k, {}), None)]

    def ts(o, i, s1, op, s2=None, op2=None):
        ins = [i] + [s for s in (s1, s2) if isinstance(s, tuple)]
        a = s1[0] if isinstance(s1, tuple) else s1
        b = s2[0] if isinstance(s2, tuple) else s2
        if op2 is None:
            issue("v", lambda: g.vector.tensor_scalar(o[0], i[0], a, None, op), [o], ins)
        else:
            issue("v", lambda: g.vector.tensor_scalar(o[0], i[0], a, b, op, op2), [o], ins)

    def tt(o, a, b, op):
        issue("v", lambda: g.vector.tensor_tensor(o[0], a[0], b[0], op), [o], [a, b])

    def cp(o, i):
        issue("v", lambda: g.vector.tensor_copy(o[0], i[0]), [o], [i])

    def ms(o, x):
        issue("v", lambda: g.vector.memset(o[0], x), [o], [])

    def act(o, i, f=F.Identity, bias=0.0, scale=1.0, acc=None):
        ins = [i] + ([bias] if isinstance(bias, tuple) else [])
        b = bias[0] if isinstance(bias, tuple) else bias
        if acc is None:
            issue("c", lambda: g.scalar.activation(o[0], i[0], f, bias=b, scale=scale), [o], ins)
        else:
            issue("c", lambda: g.scalar.activation(o[0], i[0], f, bias=b, scale=scale, accum_out=acc[0]), [o, acc], ins)

    def mm(o, l, x, start, stop):
        issue("t", lambda: g.tensor.matmul(o[0], l[0], x[0], start, stop), [o], [l, x])

    def iota(o, pat, base, cm, f=False):
        if f:
            issue("g", lambda: g.iota(o[0], pat, base, cm, allow_small_or_imprecise_dtypes=True), [o], [])
        else:
            issue("g", lambda: g.iota(o[0], pat, base, cm), [o], [])

    def aff(o, i, pat, base, cm, op=O.is_ge):
        issue("g", lambda: g.affine_select(o[0], i[0], pat, op, 0.0, base, cm), [o], [i])

    def gat(q, o, w, l, add=None):
        if q == "v":
            if add is None:
                cp(o, ind(w, l))
            else:
                ts(o, ind(w, l), add, O.add)
        else:
            act(o, ind(w, l), F.Identity, 0.0 if add is None else add)

    def scan(o, d0, d1, init, o0, o1):
        issue("v", lambda: g.vector.tensor_tensor_scan(o[0], d0[0], d1[0], init, o0, o1), [o], [d0, d1])

    def trn(o, i):
        issue("v", lambda: g.vector.transpose(o[0], i[0]), [o], [i])

    def col(k):
        return c("COL", k, k + 1)

    def sel(z, a):
        return c(z, 15 - a, 143 - a)

    def stp(n, lo, hi, step):
        return r(n, slice(None), slice(lo, hi, step))
    A_ = slice(None)
    SHR, AND = O.logical_shift_right, O.bitwise_and

    dma("y", r("CI"), r("cx")); dma("c", r("TGL"), r("tg")); dma("y", c("V", 0, 4096), r("xr")); dma("g", c("YQ", 0, 256), r("qx"))
    dma("y", r("XLH"), r("xl"))

    iota(c("IP", 0, 1), [[1, 1]], 0, 1)
    iota(r("NM"), [[1, 256]], 0, 256)
    iota(r("J16"), [[1, 16]], 0, 0, True)
    iota(r("I8"), [[16, 8]], 0, 0, True)
    ms(r("ON128"), 1.0)
    dma("y", r("LFH"), r("lf"), after=c("V", 0, 4096))
    for j in range(4):
        ts(c("DI", (5 + j) * 256, (6 + j) * 256), r("NM"), 3 * j, SHR, 7, AND)
    ts(c("DG", 1280, 2304), c("DI", 1280, 2304), 0.0625, O.mult)
    cp(r("CU"), r("CI"))
    cp(c("CF", 0, 256), r("CI"))
    ts(c("Q", 0, 256), c("YQ", 0, 256), 192.0, O.add)
    for j in range(4):
        ts(c("DI", j * 256, (j + 1) * 256), r("TGL"), 1 + 3 * j, SHR, 7, AND)
    ts(c("DI", 1024, 1280), r("TGL"), 1, AND)
    ts(c("DG", 0, 1280), c("DI", 0, 1280), 0.0625, O.mult)
    aff(r("BO1"), r("ON128"), [[-16, 8], [0, 16]], 0, 1)
    aff(r("BO"), r("BO1"), [[16, 8], [0, 16]], 15, -1)
    aff(r("IDF"), r("ON128"), [[-1, 128]], 0, 1, O.is_equal)
    aff(r("LTF"), r("BO"), [[1, 128]], -1, -1)
    iota(r("NB"), [[1, 64]], 0, 64)
    iota(r("PJ"), [[1, 8]], 0, 8)
    iota(c("CB", 0, SUMV), [[16, SUMV]], 256, 0, True)
    iota(c("CB", SUMV, 8), [[32, 8 - SUMV]], 32 * SUMV, 0, True)
    for src, b, s in ((1, "XL0", "ax0"), (2, "XL1", "ax1"), (3, "XL2", "ax2"), (1, "U0", "af0"), (2, "U1", "af1"), (3, "U2", "af2"), (1, "LFF", "aff")):
        lands(c(b, 0, 1024), s, rank + src)
    for k, src in enumerate((1, 2, 1, 3, 2, 3)):
        lands(r("E%d" % k), "ae%d" % k, rank + src)
    iota(c("Q", 256, 384), [[0, 128]], 192, 0, True); iota(c("CF", 256, 384), [[0, 128]], 0, 0, True)
    for k in range(3):
        iota(c("LF%d" % k, 1024, 1152), [[0, 128]], 0, 0)
        iota(c("XL%d" % k, 1024, 1152), [[0, 128]], 0, 0, True)
    iota(c("DD", 256, 384), [[0, 128]], 0, 0, True)
    iota(c("BA", 256, 384), [[0, 128]], 0, 0)
    iota(r("DIG"), [[0, 1024]], 0, 0, True)
    send(rank + 3, ("XL0", 1024), r("XLH"), "ax0")

    def digits():
        for f in (5, 6, 7, 8, 0, 1, 2, 3, 4):
            dma("g", r("V", slice(f, None, 16), slice(0, 4096)), c("DG", f * 256, f * 256 + 256), True, rows="V")
            if f == 0:
                cp(r("HU"), r("LFH"))
                send(rank + 3, ("U0", 1024), r("HU"), "af0")
        send(rank + 2, ("U1", 1024), r("HU"), "af1", r("U0"))
        send(rank + 2, ("XL1", 1024), r("XLH"), "ax1")
    B24 = 16777216.0

    def total_of(o, a, b):
        tmp = c("TF4", 32, 32 + int(a[0].shape[1]))
        tt(tmp, a, b, O.mult)
        issue("v", lambda: g.vector.tensor_reduce(o[0], tmp[0], AxisListType.X, O.add), [o], [tmp])

    def scaled(o, i, w):
        if isinstance(w, tuple):
            issue("c", lambda: g.scalar.activation(o[0], i[0], F.Copy, scale=w[0]), [o], [i, w])
        else:
            act(o, i, F.Copy, 0.0, float(w))

    def zbuf(n, w):
        scaled(stp(n, 15, 143, 16), stp("BO", 0, 128, 16), w)
    ms(r("ZK"), 0.0)
    scaled(r("ID"), r("IDF"), 1.0); scaled(r("NID"), r("IDF"), -1.0)
    zbuf("ZK", 65536)

    def consts():
        ts(c("IP", 1, 2), c("IP", 0, 1), 15, AND)
        ts(c("IP", 2, 3), c("IP", 0, 1), 4, SHR, 1, AND)
        cp(col(0), c("IP", 1, 2)); cp(col(1), c("IP", 2, 3))
        ts(col(20), col(1), B24, O.mult)
        ts(col(21), col(1), -B24, O.mult, B24, O.add)
        ts(col(24), col(0), 4096.0, O.mult)
        tt(col(2), col(24), col(20), O.add); tt(col(3), col(24), col(21), O.add)
        act(r("CE"), c("CF", 0, 256), F.Identity, col(2)); act(r("CO"), c("CF", 0, 256), F.Identity, col(3))
        for n in ("ZKN", "ZT", "ZTN", "ZN", "Z1"):
            ms(r(n), 0.0)
        ts(c("TF4", 0, 16), r("J16"), col(0), O.is_equal)
        ms(c("TF4", 16, 32), 0.5); ms(c("TF4", 64, 80), 0.0)
        scan(c("POW", 0, 16), c("TF4", 16, 32), c("TF4", 64, 80), 65536.0, O.mult, O.add)
        for j in range(4):
            ms(c("POW", 16 + j, 17 + j), 16.0 * 8 ** j)
        total_of(col(4), c("TF4", 0, 4), c("POW", 16, 20)); total_of(col(5), c("TF4", 5, 9), c("POW", 16, 20)); total_of(col(7), c("TF4", 0, 16), c("POW", 0, 16))
        ts(col(6), c("TF4", 4, 5), -B24, O.mult)
        ts(col(9), col(0), 5.0, O.is_ge); ts(col(10), col(0), 4.0, O.not_equal)
        ts(c("COL", 11, 15), c("J16", 1, 5), c("TF4", 4, 5), O.mult, -0.0625, O.mult)
        ts(c("COL", 15, 19), c("J16", 2, 6), c("TF4", 4, 5), O.mult, -0.0625, O.mult)
        ts(col(19), col(4), -1.0, O.mult)
        ms(r("RST"), 0.0); ms(stp("RST", 0, 512, 32), 67108864.0)
        digits()
        zbuf("ZN", col(5)); zbuf("ZT", col(4)); zbuf("ZTN", col(19)); zbuf("ZKN", -65536); zbuf("Z1", 0.0625)
        for n, w in (("RN", col(5)), ("RE", col(6)), ("RL128", col(4)), ("RD", col(7)), ("RB", 65536.0)):
            scaled(r(n), r("BO"), w)
        scaled(r("KEEP"), r("IDF"), col(9)); scaled(r("K1"), r("IDF"), -16.0)
        ts(c("CT2", 0, 16), c("POW", 0, 16), 2.0, O.mult)
        for k in (16, 32, 64, 128):
            cp(c("CT2", k, 2 * k), c("CT2", 0, k))
        act(r("CT"), r("CT2"), F.Copy, -1048576.0)

    def consts2():
        ts(r("SW8"), r("I8"), col(0), O.add); ts(r("SC8"), r("SW8"), 0.5, O.add); ts(r("SW2"), r("SW8"), 2.0, O.mult)
        ts(r("DSC"), r("SW8"), 4096.0, O.add); ts(r("DSM"), r("SW8"), 1152.0, O.add)
        ms(r("ONE"), 1.0)

    def pads():
        for j in range(3):
            ts(c("PJD", 8 * j, 8 * j + 8), r("PJ"), 3 * j, SHR, 7 if j < 2 else 1, AND)
        ts(c("PD", 0, 24), r("PJD"), 0.0625, O.mult)
        ms(c("PD", 24, 32), 0.125); ms(c("PD", 32, 40), 0.5)
        for f, k in ((0, 0), (1, 1), (2, 2), (3, 3), (5, 0), (6, 1), (7, 2), (8, 4)):
            dma("y", r("DD", slice(f, None, 16), slice(256, 384)), c("PD", 8 * k, 8 * k + 8), rows="DD")

    def labels():
        ts(r("NB"), r("NB"), 1023, AND)
        for j in range(4):
            ts(c("NBD", 64 * j, 64 * j + 64), r("NB"), 3 * j, SHR, 7, AND)
        ts(c("NBB", 0, 256), r("NBD"), 0.0625, O.mult)
        ms(c("NBB", 256, 320), 0.0625)
        for f in range(5):
            dma("y", r("DIG", slice(f, None, 16)), c("NBB", 64 * f, 64 * f + 64), rows="DIG")
        act(c("V", 4096, 4224), c("DD", 256, 384))
        tt(r("TRI"), r("LTF"), r("K1"), O.add)
        for n in range(4):
            scaled(r("TI%d" % n), r("IDF"), 32.0 * 8 ** n); scaled(r("TJ%d" % n), r("IDF"), -32.0 * 8 ** n)

    pk = [0]

    def sub(x, q, lo, u):
        k = pk[0] % 4; pk[0] += 1
        for ii in range(8):
            o = c("ps%d" % k, ii * 64, ii * 64 + 64)
            mm(o, r("NID"), c(q, lo, lo + 64), True, False)
            mm(o, r("ID"), stp(x, 8 * u + ii, 1024, 16), False, True)
        act(r("AB%d" % k), r("ps%d" % k), F.Abs)
        return k

    def sums(k, z, o, u, first, last):
        for ii in range(8):
            mm(o, sel(z, 8 * u + ii), c("AB%d" % k, ii * 64, ii * 64 + 64), first and u == 0 and ii == 0, last and u == 1 and ii == 7)

    def tags(o, gx, xd):
        for i in range(16):
            mm(o, sel("ZT", i), stp(gx, i, 1024, 16), i == 0, False)
            mm(o, sel("ZTN", i), stp(xd, i, 1024, 16), False, i == 15)

    def earlier(eq, row, cols, nb, n):
        for b in range(nb):
            ts(r(eq, A_, b, slice(0, n - 16 * b)), c(row, 16 * b, n), c(cols, b, b + 1), O.is_equal)

    def dup_compare(row, cols):
        earlier("EQ2", row, cols, 8, 128)

    def dup_count():
        mm(c("PC", 0, 128), r("RD"), r("EQ2", A_, A_, slice(0, 16)), True, False)
        for b in range(7):
            mm(c("PC", 16 * b + 16, 128), r("RB"), r("EQ2", A_, b, slice(16, 128 - 16 * b)), False, b == 6)

    def dup_flag(o):
        tt(o, c("PC", 0, 128), c("CT2", 0, 128), O.is_ge)

    def wrap(o, z, x):
        for a in range(16):
            mm(o, sel(z, a), stp(x, a, 128, 16), a == 0, a == 15)

    def choice(t):
        win = c("V", 0, 4096)

        def take(k, a=0, b=64):
            gat("v" if CHOICE[k] == "v" or k == late and a == 0 else "c", c("XG%d" % k, 16 * a, 16 * b), win, c("CU", 64 * k + a, 64 * k + b), 192.0)
        order = [k for k in range(4) if CHOICE[k] == "v"] + [k for k in range(4) if CHOICE[k] != "v"]
        late = order[-1]
        for k in order:
            if k != late:
                take(k)
        half = HALF if t else 64
        take(late, 0, half)
        if t:
            claims1(t - 1)
            disk_write(t - 1)
            claims2(t - 1)
        lag = None
        for n, k in enumerate(order):
            for u in range(2):
                b = sub("XG%d" % k, "Q", 64 * k, u)
                if n == 0 and u == 1 and half < 64:
                    take(late, half)
                if t and n == CEAT and u == 1:
                    act(r("CE"), c("CF", 0, 256), F.Identity, col(2)); act(r("CO"), c("CF", 0, 256), F.Identity, col(3))
                if lag:
                    sums(*lag)
                lag = (b, "ZK", c("PA", 64 * k, 64 * k + 64), u, True, True)
                if t and n == CL2 and u == CU2:
                    claims4(t - 1)
            if t and n == CL1:
                claims3(t - 1)
        sums(*lag)
        if t == 0:
            consts()
            consts2()
        if t:
            wrap(c("PC", 272, 280), "Z1", "FL")

    def pick(t):
        tt(r("KEY", A_, A_, slice(0, 16)), c("PA", 0, 256), r("CE"), O.add)
        tt(r("KEY", A_, A_, slice(16, 32)), c("PA", 0, 256), r("CO"), O.add)
        trn(r("KT"), r("KEY"))
        scan(r("SCN"), r("RST"), r("KT"), 67108864.0, O.max, O.min)
        cp(r("OI"), stp("SCN", 31, 512, 32))
        ts(r("OI"), r("OI"), 4095, AND)
        cp(r("OU"), r("OI"))
        cp(r("OF"), r("OI"))
        if t:
            claims5(t - 1)
        else:
            pads()
            dma("y", r("FD"), r("fd"), after=c("V", 0, 4096))
        gat("c", r("VO"), c("V", 0, 4096), r("OU"), 192.0)
        gat("v", r("XO"), c("V", 0, 4096), r("OU"), 192.0)
        tt(c("DD", 0, 256), r("VO"), r("XO"), O.subtract)
        mm(c("PR", 0, 256), r("RN"), c("DD", 0, 256), True, True)
        mm(c("PC", 0, 256), r("RE"), c("DD", 0, 256), True, False)
        for a in range(16):
            mm(c("PT", 0, 16), sel("ZT", a), stp("DD", a, 256, 16), a == 0, a == 15)
        cp(r("OR"), c("PR", 0, 256))
        for b in range(16):
            ts(r("EQ", A_, b, slice(0, 256 - 16 * b)), c("OR", 16 * b, 256), c("OF", b, b + 1), O.is_equal)
            if b < 15:
                mm(c("PC", 16 * b + 16, 256), r("RB"), r("EQ", A_, b, slice(16, 256 - 16 * b)), False, False)
        mm(c("PC", 0, 256), r("RD"), r("EQ", A_, A_, slice(0, 16)), False, True)
        tt(r("CA"), c("PC", 0, 256), r("CT"), O.is_lt)
        scan(r("PX"), r("ONE"), r("CA"), 0.0, O.mult, O.add)
        for b in range(SUMV):
            act(c("JS", 0, 256 - 16 * b), c("PX", 16 * b, 256), F.Sign, c("SC8", b, b + 1), -1.0, c("LS", b, b + 1))
        ts(r("T2"), c("PX", 255, 256), 2.0, O.mult)
        for b in range(SUMV, 8):
            ts(c("JV", 0, 256 - 16 * b), c("PX", 16 * b, 256), c("SC8", b, b + 1), O.is_le, 2.0, O.mult)
            o, i = c("LS", b, b + 1), c("JV", 0, 256 - 16 * b)
            issue("v", lambda: g.vector.tensor_reduce(o[0], i[0], AxisListType.X, O.add), [o], [i])
        ts(r("RL"), r("SW2"), r("T2"), O.subtract, 0.0, O.max)
        tt(r("CBP"), r("CB"), r("RL"), O.add)
        ts(r("INV"), r("SW2"), r("T2"), O.is_ge, 8192.0, O.mult)
        if t:
            apply(2 * (t - 1), "LF%d" % (t % 3))
        else:
            cp(c("LF0", 0, 1024), r("U0"))
        cp(r("NA"), c("PT", 0, 16))
        gat("v", c("BA", 0, 256), c("LF%d" % (t % 3), 0, 1152), r("NA"))
        tt(r("H8"), r("LS"), r("CBP"), O.add)
        ts(r("LU"), r("H8"), 0.5, O.mult)
        gat("v", r("BI"), r("BA"), r("LU"))
        gat("c", r("CR"), r("CF"), r("LU"))
        gat("c", r("QR"), r("Q"), r("LU"))
        tt(r("SQ"), r("BI"), r("BI"), O.mult)
        cp(r("CRU"), r("CR"))
        gat("v", r("DDR"), r("DD"), r("LU"))
        wrap(c("PR", 256, 264), "ZT", "DDR")

    def translate(t):
        LF, XL = "LF%d" % (t % 3), "XL%d" % (t % 3)
        wrap(c("PC", 264, 272), "ZN", "DDR")
        mm(c("PC", 0, 128), r("RL128"), r("DDR"), True, True)
        ts(c("H", 0, 128), r("SQ"), 3, SHR)
        ts(r("S5"), r("SQ"), 5, SHR)
        ts(c("H", 128, 256), r("BI"), 37.0, O.mult, 1.0, O.add)
        tt(c("H", 0, 128), c("H", 0, 128), r("BI"), O.add)
        tt(c("H", 128, 256), c("H", 128, 256), r("S5"), O.add)
        ts(r("H"), r("H"), 4095, AND)
        cp(r("CCU"), r("H"))
        for k in range(2):
            gat("c", r("GS%d" % k), c("V", 0, 4096), c("CRU", 64 * k, 64 * k + 64))
        blk = [(0, 0), (0, 1), (1, 0), (1, 1)]

        def take(k):
            lo = 128 * blk[k][1] + 64 * blk[k][0]
            gat("v" if TRANS[k] == "v" else "c", r("XG%d" % k), c("V", 0, 4096), c("CCU", lo, lo + 64))

        def plain(k):
            ts(r("XD%d" % k), r("XG%d" % k), 192.0, O.add)

        def subs(k):
            return [sub("XD%d" % k, "QR", 64 * blk[k][0], u) for u in range(2)]
        bank = [("PC", 128, "PR", 384), ("PT", 0, "PA", 256)]

        def flush(x):
            k, bs, pos = x
            hs, w = blk[k]
            bt, t0, ba, a0 = bank[hs]
            tags(c(bt, t0 + 64 * w, t0 + 64 * w + 64), "XG%d" % k, "XD%d" % k)
            for u in range(2):
                sums(bs[u], "ZK" if w else "ZKN", c(ba, a0, a0 + 64), u, pos == 0, pos == 1)

        def decide(hs):
            bt, t0, ba, a0 = bank[hs]
            lo, hi = 64 * hs, 64 * hs + 64
            for w in range(2):
                tt(c("IN", 128 * w + lo, 128 * w + hi), c(bt, t0 + 64 * w, t0 + 64 * w + 64), c("BS", lo, hi), O.is_equal)
            ts(c("INB", lo, hi), c("IN", lo, hi), 33554432.0, O.mult)
            tt(c("M2", lo, hi), c(ba, a0, a0 + 64), c("IN", 128 + lo, 128 + hi), O.max)
            tt(c("SEL", lo, hi), c("M2", lo, hi), c("INB", lo, hi), O.is_gt)
            tt(c("SEL", lo, hi), c("SEL", lo, hi), c("D12", lo, hi), O.mult)
            tt(c("SS", lo, hi), c("SEL", lo, hi), c("H", lo, hi), O.add)
            if hs == 0:
                claim_keys(lo, hi)
            cp(ind(r("FW"), c("OUR", 4 * hs, 4 * hs + 4)), c("SS", lo, hi))
        take(0); plain(0)
        cp(r("NU"), c("PR", 256, 264))
        cp(r("OUR"), c("PC", 264, 272))
        cp(r("NR"), c("PC", 0, 128))
        take(1)
        b0 = subs(0)
        plain(1)
        take(2); take(3)
        b1 = subs(1)
        gat("c", r("A"), r(XL), r("NU"))
        flush((0, b0, 0))
        plain(2)
        b2 = subs(2)
        flush((1, b1, 1))
        plain(3)
        lag = [(3, subs(3), 1)]
        flush((2, b2, 0))
        cp(r("WNF"), r("NU"))
        tt(r("D12"), c("H", 128, 256), c("H", 0, 128), O.subtract)
        ts(r("BS"), r("BI"), -1797120.0, O.add)
        for k in range(2):
            ts(r("SX%d" % k), r("GS%d" % k), 192.0, O.add)
        if t == 0:
            labels()
            ts(c("FW", 0, 2048), r("FD"), 4095, AND)
            ts(c("FW", 2048, 4096), r("FD"), 12, SHR)
        ts(r("DDM"), r("DDR"), col(10), O.mult, col(11 + t), O.add)
        tt(r("VL"), r("A"), r("DDM"), O.add)
        cp(ind(r("V"), r("OUR")), r("VL"))
        tt(r("QF"), ind(c("V", 0, 4096), r("OU")), c("Q", 0, 256), O.add)
        ts(c("Q", 0, 256), r("QF"), 0.5, O.mult, 95.75, O.add)
        cp(r("NI"), r("NU"))
        ts(r("N1"), r("NI"), 1, AND)
        ts(r("N1"), r("N1"), -2.0, O.mult, 1.0, O.add)
        tt(r("NI"), r("NI"), r("N1"), O.add)
        decide(0)
        if t == 1:
            cp(c("LF2", 0, 1024), r("U2"))
            apply(1, "LF2")
        if t == 2:
            apply(3, "LF0")
        dup_compare("NR", "WNF")
        flush(lag.pop())
        dup_count()
        decide(1)
        if t == STEPS - 1:
            dup_flag(r("FL"))
            wrap(c("PC", 272, 280), "Z1", "FL")
            claim_order()
        for k in range(2):
            tags(c("PT", 256 + 64 * k, 320 + 64 * k), "GS%d" % k, "SX%d" % k)
        cp(c("CF", 0, 256), ind(c("FW", 0, 4096), r("OU")))
        if t < STEPS - 1:
            cp(r("CU"), c("CF", 0, 256))

    def claim_keys(lo, hi):
        tt(c("N12", lo, hi), c("IN", lo, hi), c("IN", 128 + lo, 128 + hi), O.max)
        ts(c("NEW", lo, hi), c("N12", lo, hi), -1.0, O.mult, 1.0, O.add)
        ts(c("K1", lo, hi), c("SS", lo, hi), 1024.0, O.mult)
        tt(c("KK", lo, hi), c("K1", lo, hi), c("BI", lo, hi), O.add)

    def disk_write(t):
        act(c("SF", 0, 128), c("PT", 256, 384), F.Identity, 1797120.0)
        tt(r("MF"), c("PC", 272, 280), r("DSM"), O.mult)
        tt(c("SF", 128, 136), r("MF"), r("NI"), O.max)
        for dst, k in (((3, 0), (2, 1)), ((3, 2), (1, 3)), ((2, 4),), ((1, 5),))[t]:
            send(rank + dst, ("E%d" % k, 136), r("SF"), "ae%d" % k)
        if t == 0:
            send(rank + 1, ("U2", 1024), r("HU"), "af2")
            send(rank + 1, ("XL2", 1024), r("XLH"), "ax2")
        if t in (0, 2):
            cp(r("MU"), c("SF", 128, 136))
            cp(ind(r("LF%d" % t), r("MU")), c("SF", 0, 128))
        if t == 2:
            send(rank + 3, ("LFF", 1024), c("LF2", 0, 1024), "aff")

    def apply(k, n):
        cp(r("MX"), c("E%d" % k, 128, 136))
        cp(ind(r(n), r("MX")), c("E%d" % k, 0, 128))

    def claims1(t):
        if t < STEPS - 1:
            dup_flag(r("FL"))
            wrap(c("PC", 272, 280), "Z1", "FL")
            claim_order()

    def claim_order():
        claim_keys(64, 128)
        mm(c("PC", 384, 512), r("TRI"), r("NEW"), True, True)
        act(r("KKE"), r("KK"), F.Identity, col(20)); act(r("KKO"), r("KK"), F.Identity, col(21))

    def claims2(t):
        ts(r("PEN"), c("PC", 384, 512), -16.0, O.is_gt, B24, O.mult)
        tt(r("KEC", A_, A_, slice(0, 16)), r("PEN"), r("KKE"), O.add)
        tt(r("KEC", A_, A_, slice(16, 32)), r("PEN"), r("KKO"), O.add)
        trn(r("KTC"), r("KEC"))
        scan(r("SNC"), c("RST", 0, 256), r("KTC"), 67108864.0, O.max, O.min)
        cp(r("KI"), stp("SNC", 31, 256, 32))
        ts(r("PI"), r("KI"), 10, SHR)
        ts(r("BW"), r("KI"), 1023, AND)
        tt(r("PF"), r("PI"), r("INV"), O.max)
        tt(r("PF"), r("PF"), r("DSC"), O.min)
        cp(r("PU"), r("PF"))
        cp(r("BU"), r("BW"))
        gat("v", r("GP"), r("V"), r("PU"), 192.0)
        gat("v", r("XP"), r("V"), r("PU"), 192.0)
        gat("v", r("DB"), r("DIG"), r("BU"))
        tt(r("DP"), r("GP"), r("XP"), O.subtract)
        ts(r("ZC"), r("DP"), -(t + 1) / 16.0, O.is_equal, col(15 + t), O.mult)

    def claims3(t):
        mm(c("PR", 0, 128), r("RN"), r("DP"), True, True)
        o = c("PT", 384, 512)
        mm(o, r("ID"), r("XP"), True, False); mm(o, r("KEEP"), r("DP"), False, False)
        mm(o, r("ID"), r("DB"), False, False); mm(o, r("ID"), r("ZC"), False, True)
        if t == 0:
            cp(c("LF1", 0, 1024), r("U1"))
        cp(r("PLR"), c("PR", 0, 128))
        dup_compare("PLR", "PF")
        ts(r("NV"), o, -192.0, O.add)

    def claims4(t):
        dup_count()
        dup_flag(r("FL"))

    def claims5(t):
        tt(r("FS"), c("PC", 272, 280), r("DSC"), O.mult)
        tt(r("P2"), r("FS"), r("PF"), O.max)
        cp(r("PU2"), r("P2"))
        cp(ind(r("V"), r("PU2")), r("NV"))

    for t in range(STEPS):
        choice(t)
        pick(t)
        translate(t)
    claims1(STEPS - 1)
    dma("y", r("yc"), c("CF", 0, 256))
    disk_write(STEPS - 1)
    claims2(STEPS - 1)
    ts(r("YQ"), c("Q", 0, 256), -192.0, O.add)
    dma("y", r("yq"), r("YQ"))
    claims3(STEPS - 1); claims4(STEPS - 1)
    wrap(c("PC", 272, 280), "Z1", "FL")
    claims5(STEPS - 1)
    for n in range(5):
        dma("y" if n % 2 else "c", c("TX", 256 * n, 256 * n + 256), r("V", slice(n, None, 16), slice(0, 4096)))
    cp(c("YL", 0, 1024), c("LFF", 0, 1024))
    apply(5, "YL")
    dma("y", r("yl"), c("YL", 0, 1024))
    ts(r("TD"), r("TX"), 192.0, O.add)
    for n in range(4):
        mm(c("PT", 0, 256), r("TI%d" % n), c("TX", 256 * n, 256 * n + 256), n == 0, False)
        mm(c("PT", 0, 256), r("TJ%d" % n), c("TD", 256 * n, 256 * n + 256), False, n == 3)
    act(r("TE"), c("TX", 1024, 1280), F.Identity, 192.0625)
    tt(r("TE2"), r("TE"), c("TD", 1024, 1280), O.subtract)
    ts(r("TE2"), r("TE2"), 0.125, O.is_equal, 3594240.0, O.add)
    tt(r("TY"), c("PT", 0, 256), r("TE2"), O.add)
    dma("c", r("yt"), r("TY"))
    for s in sorted(total):
        g.wait_ge(T.sem[s], total[s])
